import numpy as np
import ml_dtypes


def mxq(x, axis, fmt="e4m3"):
    dtype, down = {"e4m3": (ml_dtypes.float8_e4m3fn, 7), "e5m2": (ml_dtypes.float8_e5m2, 14)}[fmt]
    v = np.moveaxis(np.asarray(x, np.float32).astype(ml_dtypes.bfloat16).astype(np.float64), axis, -1)
    blocks = v.reshape(v.shape[:-1] + (-1, 32))
    amax = np.abs(blocks).max(-1, keepdims=True)
    byte = np.maximum(np.where(amax > 0, np.frexp(amax)[1] - 1 + 127, 0) - down, 1)
    scale = np.exp2(byte - 127.0)
    codes = (blocks / scale).astype(np.float32).astype(dtype).astype(np.float64)
    return np.moveaxis((codes * scale).reshape(v.shape), -1, axis)


WIDE = False


def mx_kscale(k):
    if not WIDE:
        return np.ones(k)
    levels = np.array([10, -10, 5, -5, 0])
    if k % 512:
        return np.exp2(np.random.permutation(np.resize(levels, k // 32))).repeat(32)
    a = np.empty((k // 512, 16))
    for p in range(k // 512):
        a[p, :8] = np.random.permutation(np.resize(levels, 8))
        for g in range(8):
            far = levels[np.abs(levels - a[p, g]) >= 10]
            a[p, g + 8] = far[np.random.randint(len(far))]
    return np.exp2(a.ravel()).repeat(32)


def f64(x):
    return np.asarray(x).astype(np.float64)


def striped(idx):
    return np.tile(np.asarray(idx).reshape(-1, 16).T, (8, 1)).astype(np.uint16)


def unstriped(offs):
    return offs[:16].T.reshape(-1).astype(np.int64)


E2M1 = np.array([0.0, 0.5, 1.0, 1.5, 2.0, 3.0, 4.0, 6.0, -0.0, -0.5, -1.0, -1.5, -2.0, -3.0, -4.0, -6.0])


def pack_weight(w, fmt):
    k, n = w.shape
    w = f64(np.asarray(w, np.float32).astype(ml_dtypes.bfloat16)).reshape(k // 32, 32, n)
    amax = np.abs(w).max(1)
    if fmt == "e4m3":
        byte = np.frexp(amax)[1] - 1 + 127 - 7
    else:
        mant, ex = np.frexp(amax / 6.0)
        byte = np.where(mant > 0.5, ex, ex - 1) + 127
    byte = np.clip(np.where(amax > 0, byte, 1), 1, 254)
    scaled = (w * np.exp2(127.0 - byte)[:, None, :]).reshape(k, n).astype(np.float32)
    by_word = np.ascontiguousarray(scaled.reshape(k // 512, 128, 4, n).transpose(0, 1, 3, 2))
    if fmt == "e4m3":
        words = by_word.astype(ml_dtypes.float8_e4m3fn).view(np.uint8)
    else:
        c = by_word.astype(ml_dtypes.float4_e2m1fn).view(np.uint8) & 0xF
        words = (c[..., 0::2] | (c[..., 1::2] << 4)).reshape(k // 512, 128, 2 * n)
    return np.ascontiguousarray(words), np.ascontiguousarray(byte.astype(np.uint8).reshape(k // 512, 16, n))


def unpack_weight(words, scales, fmt):
    g, _, n = scales.shape
    words = np.ascontiguousarray(words).reshape(g, 128, n, -1)
    if fmt == "e4m3":
        vals = words.view(ml_dtypes.float8_e4m3fn).astype(np.float64)
    else:
        nib = np.empty((g, 128, n, 4), np.uint8)
        nib[..., 0::2] = words & 0xF
        nib[..., 1::2] = words >> 4
        vals = E2M1[nib]
    vals = vals * np.repeat(np.exp2(scales.astype(np.float64) - 127.0), 8, axis=1)[..., None]
    return vals.transpose(0, 1, 3, 2).reshape(g * 512, n)


B, N, T, D, NQ = 1, 512, 2048, 1024, 256
SEG = 8


def setup_inputs():
    n = np.random.standard_normal
    idx = np.random.permutation(T)[:B * N]
    s = mx_kscale(D)[:, None]
    kp = pack_weight(n((D, T)) / s, "e2m1")
    return {
        "qT": (n((B, D, NQ)) * s * (1.00 / np.sqrt(D))).astype(np.float32),
        "k_words": np.ascontiguousarray(kp[0].reshape(1, 2, 128, T, 2).transpose(0, 2, 3, 1, 4)).reshape(1, 128, T, 4),
        "k_scales": kp[1],
        "kb": np.tile(n(2048), (128, 1)).astype(np.float32),
        "offs": striped(idx),
    }


def reference(qT, k_words, k_scales, kb, offs):
    idx = unstriped(offs)
    pick = lambda x, which: x[:, which].reshape(x.shape[0], B, -1).transpose(1, 0, 2)
    k = unpack_weight(k_words.reshape(1, 128, T, 2, 2).transpose(0, 3, 1, 2, 4).reshape(2, 128, 2 * T), k_scales, "e2m1")
    kg = pick(k, idx)
    qq = mxq(f64(qT), 1, "e4m3")
    a = qq.transpose(0, 2, 1) @ kg
    y = np.log(1.0 + np.maximum(a + pick(f64(kb), idx)[:, :1, :], 0.0)).reshape(B, NQ, N // SEG, SEG).max(-1)
    return y

@@ -1,0 +1,158 @@
+from contextlib import ExitStack
+
+import concourse.mybir as mybir
+from concourse.masks import make_identity
+
+F32 = mybir.dt.float32
+BF16 = mybir.dt.bfloat16
+I32 = mybir.dt.int32
+U32 = mybir.dt.uint32
+U16 = mybir.dt.uint16
+U8 = mybir.dt.uint8
+FP8X4 = mybir.dt.float8_e4m3fn_x4
+FP4X4 = mybir.dt.float4_e2m1fn_x4
+ACT = mybir.ActivationFunctionType
+ALU = mybir.AluOpType
+
+P = 128
+PACK = 4
+PASSES = 2
+D = 1024
+NQ = 256
+N = 512
+T = 2048
+SEG = 8
+HALF = N // 2
+
+FLOPS = 2 * NQ * N * D
+BYTES = D * NQ * 4 + P * T * 4 + PASSES * 16 * T + T * 4 + P * (N // 16) * 2 + NQ * (N // SEG) * 4
+
+
+def tile_attend_splade_topk_kernel(tc, qT, k_words, k_scales, kb, offs, out):
+    nc = tc.nc
+    with ExitStack() as ctx:
+        sb = ctx.enter_context(tc.tile_pool(name="sb", bufs=1))
+        ps = ctx.enter_context(tc.psum_pool(name="ps", bufs=1))
+
+        offsets = sb.tile([P, N // 16], U16, name="offsets")
+        nc.sync.dma_start(offsets[:], offs)
+
+        scale_pool = sb.tile([P, T], U8, name="scale_pool", align_bytes=64)
+        nc.sync.dma_start(
+            out=scale_pool[96:P, :].bitcast(I32),
+            in_=k_scales.bitcast(I32).rearrange("o f t -> f o t"),
+        )
+        nc.vector.memset(scale_pool[0:96, :].bitcast(I32), 0)
+
+        bias_pool = sb.tile([P, T], F32, name="bias_pool")
+        nc.sync.dma_start(out=bias_pool[P - 1 : P, :], in_=kb[0:1, :])
+        nc.vector.memset(bias_pool[0 : P - 1, :], 0.0)
+
+        q_raw = [sb.tile([P, PACK, NQ], F32, name=f"q_raw{o}") for o in range(PASSES)]
+        word_pool = sb.tile([P, T], U32, name="word_pool")
+        q_rows = qT[0].rearrange("(o p j) w -> o p j w", o=PASSES, j=PACK)
+        nc.sync.dma_start(out=q_raw[0][:], in_=q_rows[0])
+        nc.sync.dma_start(out=word_pool[:].bitcast(I32), in_=k_words[0].rearrange("p t b -> p (t b)").bitcast(I32))
+        nc.sync.dma_start(out=q_raw[1][:], in_=q_rows[1])
+
+        ident = sb.tile([P, P], F32, name="ident")
+        make_identity(nc, ident[:])
+        warm = sb.tile([P, 1], F32, name="warm")
+        nc.scalar.activation(warm[:], ident[:, 0:1], ACT.Ln, bias=1.0)
+
+        k_scale = sb.tile([P, PASSES * N], U8, name="k_scale", align_bytes=64)
+        nc.vector.memset(k_scale[:].bitcast(I32), 0)
+        scale_rows = sb.tile([P, N], U8, name="scale_rows", align_bytes=64)
+        nc.vector.tensor_copy(scale_rows[:], scale_pool[:].indirect(offsets[:]))
+        for quad in range(4):
+            nc.scalar.dma_start(
+                out=k_scale[32 * quad : 32 * quad + 4, :].bitcast(I32),
+                in_=scale_rows[96 + 8 * quad : 96 + 8 * quad + 8, :].bitcast(I32),
+            )
+
+        bias_row = sb.tile([P, N], F32, name="bias_row")
+        nc.vector.tensor_copy(bias_row[:], bias_pool[:].indirect(offsets[:]))
+        bias_ps = ps.tile([P, 4, P], F32, name="bias_ps", tag="bank7")
+        for s in range(4):
+            nc.tensor.transpose(bias_ps[:, s, :], bias_row[:, s * P : (s + 1) * P], ident[:])
+        bias_col = sb.tile([P, 4], F32, name="bias_col")
+        nc.scalar.copy(out=bias_col[:], in_=bias_ps[:, :, P - 1])
+
+        def quantise(o, c0, width):
+            grouped = sb.tile([P, width, PACK], BF16, name=f"q_bf{o}_{c0}", align_bytes=64)
+            nc.scalar.copy(
+                out=grouped[:].rearrange("p (c i) t -> p c t i", i=4),
+                in_=q_raw[o][:, :, c0 : c0 + width].rearrange("p t (c i) -> p c t i", i=4),
+            )
+            codes = sb.tile([P, width], U32, name=f"q_codes{o}_{c0}", align_bytes=64)
+            plane = sb.tile([P, width], U8, name=f"q_scale{o}_{c0}", align_bytes=64)
+            nc.vector.quantize_mx(out=codes[:].bitcast(FP8X4), scales=plane[:], in_=grouped[:].rearrange("p w t -> p (w t)"))
+            return codes, plane
+
+        codes0, plane0 = quantise(0, 0, NQ)
+
+        pairs = sb.tile([P, N], U32, name="pairs", align_bytes=64)
+        halves = pairs[:].bitcast(U16).rearrange("p (n o) -> p o n", o=PASSES)
+        low = []
+        for u in range(2):
+            nc.vector.tensor_copy(pairs[:, u * HALF : (u + 1) * HALF], word_pool[:].indirect(offsets[:, 16 * u : 16 * (u + 1)]))
+            part = sb.tile([P, 2 * HALF], U8, name=f"low{u}", align_bytes=64)
+            nc.vector.tensor_copy(out=part[:].bitcast(U16), in_=halves[:, 0, u * HALF : (u + 1) * HALF])
+            low.append(part)
+
+        banks = {}
+        for s in range(4):
+            for h in range(2):
+                bank = ps.tile([P, P], F32, name=f"score{s}{h}", tag=f"bank{4 * h + s}")
+                banks[s, h] = bank
+                nc.tensor.matmul_mx(
+                    out=bank[:],
+                    lhsT=low[s // 2][:, 2 * P * (s % 2) : 2 * P * (s % 2 + 1)].bitcast(FP4X4),
+                    lhsT_scale=k_scale[:, s * P : (s + 1) * P],
+                    rhs=codes0[:, h * P : (h + 1) * P].bitcast(FP8X4),
+                    rhs_scale=plane0[:, h * P : (h + 1) * P],
+                    start=True,
+                    stop=False,
+                )
+
+        second = [quantise(1, 0, P)]
+        high = sb.tile([P, 2 * N], U8, name="high", align_bytes=64)
+        nc.vector.tensor_copy(out=high[:].bitcast(U16), in_=halves[:, 1, :])
+        second.append(quantise(1, P, P))
+
+        acts = {}
+        for h in range(2):
+            codes1, plane1 = second[h]
+            for s in range(4):
+                nc.tensor.matmul_mx(
+                    out=banks[s, h][:],
+                    lhsT=high[:, 2 * P * s : 2 * P * (s + 1)].bitcast(FP4X4),
+                    lhsT_scale=k_scale[:, N + s * P : N + (s + 1) * P],
+                    rhs=codes1[:].bitcast(FP8X4),
+                    rhs_scale=plane1[:],
+                    start=False,
+                    stop=True,
+                )
+                act = sb.tile([P, P], F32, name=f"act{s}{h}")
+                if s % 2 == 0:
+                    nc.vector.tensor_scalar(act[:], banks[s, h][:], bias_col[:, s : s + 1], 0.0, ALU.add, ALU.max)
+                else:
+                    nc.scalar.activation(act[:], banks[s, h][:], ACT.Relu, bias=bias_col[:, s : s + 1])
+                acts[s, h] = act
+
+        best = sb.tile([P, 2, N // SEG], F32, name="best")
+        for n, (h, group) in enumerate(((0, (0, 1, 2, 3)), (1, (0, 1)), (1, (2, 3)))):
+            turned = ps.tile([P, len(group) * P], F32, name=f"turned{n}", tag=f"bank{n}")
+            for i, s in enumerate(group):
+                nc.tensor.transpose(turned[:, i * P : (i + 1) * P], acts[s, h][:], ident[:])
+            j0 = group[0] * (P // SEG)
+            nc.vector.tensor_reduce(
+                out=best[:, h, j0 : j0 + len(group) * (P // SEG)],
+                in_=turned[:].rearrange("p (j e) -> p j e", e=SEG),
+                axis=mybir.AxisListType.X,
+                op=ALU.max,
+            )
+
+        result = sb.tile([P, 2, N // SEG], F32, name="result")
+        nc.scalar.activation(result[:], best[:], ACT.Ln, bias=1.0)
+        nc.sync.dma_start(out=out[0].rearrange("(h p) j -> p h j", p=P), in_=result[:])

@@ -34,6 +34,13 @@ def tile_attend_splade_topk_kernel(tc, qT, k_words, k_scales, kb, offs, out):
         sb = ctx.enter_context(tc.tile_pool(name="sb", bufs=1))
         ps = ctx.enter_context(tc.psum_pool(name="ps", bufs=1))
 
+        ident = sb.tile([P, P], F32, name="ident")
+        make_identity(nc, ident[:])
+        zero = sb.tile([P, 1], F32, name="zero")
+        nc.vector.memset(zero[:], 0.0)
+        warm = sb.tile([P, 1], F32, name="warm")
+        nc.scalar.activation(warm[:], zero[:], ACT.Ln, bias=1.0)
+
         offsets = sb.tile([P, N // 16], U16, name="offsets")
         nc.sync.dma_start(offsets[:], offs)
 
@@ -44,21 +51,16 @@ def tile_attend_splade_topk_kernel(tc, qT, k_words, k_scales, kb, offs, out):
         )
         nc.vector.memset(scale_pool[0:96, :].bitcast(I32), 0)
 
-        bias_pool = sb.tile([P, T], F32, name="bias_pool")
+        bias_pool = sb.tile([P, T], F32, name="bias_pool", tag="bias_then_pairs", align_bytes=64)
         nc.sync.dma_start(out=bias_pool[P - 1 : P, :], in_=kb[0:1, :])
-        nc.vector.memset(bias_pool[0 : P - 1, :], 0.0)
+        nc.vector.memset(bias_pool[0 : P - 1, :].bitcast(I32), 0)
 
-        q_raw = [sb.tile([P, PACK, NQ], F32, name=f"q_raw{o}") for o in range(PASSES)]
+        q_raw = [sb.tile([P, PACK, NQ], F32, name=f"q_raw{o}", tag=f"q_raw{o}", align_bytes=64) for o in range(PASSES)]
         word_pool = sb.tile([P, T], U32, name="word_pool")
         q_rows = qT[0].rearrange("(o p j) w -> o p j w", o=PASSES, j=PACK)
-        nc.sync.dma_start(out=q_raw[0][:], in_=q_rows[0])
         nc.sync.dma_start(out=word_pool[:].bitcast(I32), in_=k_words[0].rearrange("p t b -> p (t b)").bitcast(I32))
+        nc.sync.dma_start(out=q_raw[0][:], in_=q_rows[0])
         nc.sync.dma_start(out=q_raw[1][:], in_=q_rows[1])
-
-        ident = sb.tile([P, P], F32, name="ident")
-        make_identity(nc, ident[:])
-        warm = sb.tile([P, 1], F32, name="warm")
-        nc.scalar.activation(warm[:], ident[:, 0:1], ACT.Ln, bias=1.0)
 
         k_scale = sb.tile([P, PASSES * N], U8, name="k_scale", align_bytes=64)
         nc.vector.memset(k_scale[:].bitcast(I32), 0)
@@ -70,89 +72,74 @@ def tile_attend_splade_topk_kernel(tc, qT, k_words, k_scales, kb, offs, out):
                 in_=scale_rows[96 + 8 * quad : 96 + 8 * quad + 8, :].bitcast(I32),
             )
 
-        bias_row = sb.tile([P, N], F32, name="bias_row")
+        bias_row = sb.tile([P, N], F32, name="bias_row", tag="q_bf10", align_bytes=64)
         nc.vector.tensor_copy(bias_row[:], bias_pool[:].indirect(offsets[:]))
-        bias_ps = ps.tile([P, 4, P], F32, name="bias_ps", tag="bank7")
+        bias_ps = ps.tile([P, 4, P], F32, name="bias_ps", tag="bank0")
         for s in range(4):
             nc.tensor.transpose(bias_ps[:, s, :], bias_row[:, s * P : (s + 1) * P], ident[:])
         bias_col = sb.tile([P, 4], F32, name="bias_col")
         nc.scalar.copy(out=bias_col[:], in_=bias_ps[:, :, P - 1])
 
-        def quantise(o, c0, width):
-            grouped = sb.tile([P, width, PACK], BF16, name=f"q_bf{o}_{c0}", align_bytes=64)
-            nc.scalar.copy(
-                out=grouped[:].rearrange("p (c i) t -> p c t i", i=4),
-                in_=q_raw[o][:, :, c0 : c0 + width].rearrange("p t (c i) -> p c t i", i=4),
-            )
-            codes = sb.tile([P, width], U32, name=f"q_codes{o}_{c0}", align_bytes=64)
-            plane = sb.tile([P, width], U8, name=f"q_scale{o}_{c0}", align_bytes=64)
-            nc.vector.quantize_mx(out=codes[:].bitcast(FP8X4), scales=plane[:], in_=grouped[:].rearrange("p w t -> p (w t)"))
-            return codes, plane
-
-        codes0, plane0 = quantise(0, 0, NQ)
-
-        pairs = sb.tile([P, N], U32, name="pairs", align_bytes=64)
+        pairs = sb.tile([P, N], U32, name="pairs", tag="bias_then_pairs", align_bytes=64)
+        nc.vector.tensor_copy(pairs[:], word_pool[:].indirect(offsets[:]))
         halves = pairs[:].bitcast(U16).rearrange("p (n o) -> p o n", o=PASSES)
-        low = []
-        for u in range(2):
-            nc.vector.tensor_copy(pairs[:, u * HALF : (u + 1) * HALF], word_pool[:].indirect(offsets[:, 16 * u : 16 * (u + 1)]))
-            part = sb.tile([P, 2 * HALF], U8, name=f"low{u}", align_bytes=64)
-            nc.vector.tensor_copy(out=part[:].bitcast(U16), in_=halves[:, 0, u * HALF : (u + 1) * HALF])
-            low.append(part)
 
         banks = {}
-        for s in range(4):
+        q_mx = {}
+        k_codes = []
+        for o in range(PASSES):
+            part = sb.tile([P, 2 * N], U8, name=f"k_codes{o}", tag=("k_low", "q_raw0")[o], align_bytes=64)
+            nc.vector.tensor_copy(out=part[:].bitcast(U16), in_=halves[:, o, :])
+            k_codes.append(part)
             for h in range(2):
-                bank = ps.tile([P, P], F32, name=f"score{s}{h}", tag=f"bank{4 * h + s}")
-                banks[s, h] = bank
-                nc.tensor.matmul_mx(
-                    out=bank[:],
-                    lhsT=low[s // 2][:, 2 * P * (s % 2) : 2 * P * (s % 2 + 1)].bitcast(FP4X4),
-                    lhsT_scale=k_scale[:, s * P : (s + 1) * P],
-                    rhs=codes0[:, h * P : (h + 1) * P].bitcast(FP8X4),
-                    rhs_scale=plane0[:, h * P : (h + 1) * P],
-                    start=True,
-                    stop=False,
+                grouped = sb.tile([P, P, PACK], BF16, name=f"q_bf{o}{h}", tag=f"q_bf{o}{h}", align_bytes=64)
+                nc.scalar.copy(
+                    out=grouped[:].rearrange("p (c i) t -> p c t i", i=4),
+                    in_=q_raw[o][:, :, h * P : (h + 1) * P].rearrange("p t (c i) -> p c t i", i=4),
                 )
-
-        second = [quantise(1, 0, P)]
-        high = sb.tile([P, 2 * N], U8, name="high", align_bytes=64)
-        nc.vector.tensor_copy(out=high[:].bitcast(U16), in_=halves[:, 1, :])
-        second.append(quantise(1, P, P))
+                codes = sb.tile([P, P], U32, name=f"q_codes{o}{h}", align_bytes=64)
+                plane = sb.tile([P, P], U8, name=f"q_scale{o}{h}", align_bytes=64)
+                nc.vector.quantize_mx(out=codes[:].bitcast(FP8X4), scales=plane[:], in_=grouped[:].rearrange("p w t -> p (w t)"))
+                q_mx[o, h] = codes, plane
 
         acts = {}
+        for o in range(PASSES):
+            for h in range(2):
+                codes, plane = q_mx[o, h]
+                for s in range(4):
+                    if o == 0:
+                        banks[s, h] = ps.tile([P, P], F32, name=f"score{s}{h}", tag=f"bank{4 * h + s}")
+                    nc.tensor.matmul_mx(
+                        out=banks[s, h][:],
+                        lhsT=k_codes[o][:, 2 * P * s : 2 * P * (s + 1)].bitcast(FP4X4),
+                        lhsT_scale=k_scale[:, o * N + s * P : o * N + (s + 1) * P],
+                        rhs=codes[:].bitcast(FP8X4),
+                        rhs_scale=plane[:],
+                        start=(o == 0),
+                        stop=(o == 1),
+                    )
+                    if o == 1:
+                        act = sb.tile([P, P], F32, name=f"act{s}{h}")
+                        if h == 1 and s % 2 == 0:
+                            nc.vector.tensor_scalar(act[:], banks[s, h][:], bias_col[:, s : s + 1], 0.0, ALU.add, ALU.max)
+                        else:
+                            nc.scalar.activation(act[:], banks[s, h][:], ACT.Relu, bias=bias_col[:, s : s + 1])
+                        acts[s, h] = act
+
         for h in range(2):
-            codes1, plane1 = second[h]
-            for s in range(4):
-                nc.tensor.matmul_mx(
-                    out=banks[s, h][:],
-                    lhsT=high[:, 2 * P * s : 2 * P * (s + 1)].bitcast(FP4X4),
-                    lhsT_scale=k_scale[:, N + s * P : N + (s + 1) * P],
-                    rhs=codes1[:].bitcast(FP8X4),
-                    rhs_scale=plane1[:],
-                    start=False,
-                    stop=True,
+            best = sb.tile([P, N // SEG], F32, name=f"best{h}")
+            groups = ((0, 1, 2, 3),) if h == 0 else ((0, 1), (2, 3))
+            for group in groups:
+                turned = ps.tile([P, len(group) * P], F32, name=f"turned{h}{group[0]}", tag=f"bank{h + group[0] // 2}")
+                for i, s in enumerate(group):
+                    nc.tensor.transpose(turned[:, i * P : (i + 1) * P], acts[s, h][:], ident[:])
+                j0 = group[0] * (P // SEG)
+                nc.vector.tensor_reduce(
+                    out=best[:, j0 : j0 + len(group) * (P // SEG)],
+                    in_=turned[:].rearrange("p (j e) -> p j e", e=SEG),
+                    axis=mybir.AxisListType.X,
+                    op=ALU.max,
                 )
-                act = sb.tile([P, P], F32, name=f"act{s}{h}")
-                if s % 2 == 0:
-                    nc.vector.tensor_scalar(act[:], banks[s, h][:], bias_col[:, s : s + 1], 0.0, ALU.add, ALU.max)
-                else:
-                    nc.scalar.activation(act[:], banks[s, h][:], ACT.Relu, bias=bias_col[:, s : s + 1])
-                acts[s, h] = act
-
-        best = sb.tile([P, 2, N // SEG], F32, name="best")
-        for n, (h, group) in enumerate(((0, (0, 1, 2, 3)), (1, (0, 1)), (1, (2, 3)))):
-            turned = ps.tile([P, len(group) * P], F32, name=f"turned{n}", tag=f"bank{n}")
-            for i, s in enumerate(group):
-                nc.tensor.transpose(turned[:, i * P : (i + 1) * P], acts[s, h][:], ident[:])
-            j0 = group[0] * (P // SEG)
-            nc.vector.tensor_reduce(
-                out=best[:, h, j0 : j0 + len(group) * (P // SEG)],
-                in_=turned[:].rearrange("p (j e) -> p j e", e=SEG),
-                axis=mybir.AxisListType.X,
-                op=ALU.max,
-            )
-
-        result = sb.tile([P, 2, N // SEG], F32, name="result")
-        nc.scalar.activation(result[:], best[:], ACT.Ln, bias=1.0)
-        nc.sync.dma_start(out=out[0].rearrange("(h p) j -> p h j", p=P), in_=result[:])
+            result = sb.tile([P, N // SEG], F32, name=f"result{h}")
+            nc.scalar.activation(result[:], best[:], ACT.Ln, bias=1.0)
+            nc.sync.dma_start(out=out[0, h * P : (h + 1) * P, :], in_=result[:])

@@ -44,8 +44,8 @@ def tile_attend_splade_topk_kernel(tc, qT, k_words, k_scales, kb, offs, out):
         offsets = sb.tile([P, N // 16], U16, name="offsets")
         nc.sync.dma_start(offsets[:], offs)
 
-        scale_pool = sb.tile([P, T], U8, name="scale_pool", align_bytes=64)
-        nc.sync.dma_start(
+        scale_pool = sb.tile([P, T], U8, name="scale_pool", tag="scales_then_q", align_bytes=64)
+        nc.scalar.dma_start(
             out=scale_pool[96:P, :].bitcast(I32),
             in_=k_scales.bitcast(I32).rearrange("o f t -> f o t"),
         )
@@ -55,12 +55,14 @@ def tile_attend_splade_topk_kernel(tc, qT, k_words, k_scales, kb, offs, out):
         nc.sync.dma_start(out=bias_pool[P - 1 : P, :], in_=kb[0:1, :])
         nc.vector.memset(bias_pool[0 : P - 1, :].bitcast(I32), 0)
 
-        q_raw = [sb.tile([P, PACK, NQ], F32, name=f"q_raw{o}", tag=f"q_raw{o}", align_bytes=64) for o in range(PASSES)]
         word_pool = sb.tile([P, T], U32, name="word_pool")
-        q_rows = qT[0].rearrange("(o p j) w -> o p j w", o=PASSES, j=PACK)
         nc.sync.dma_start(out=word_pool[:].bitcast(I32), in_=k_words[0].rearrange("p t b -> p (t b)").bitcast(I32))
-        nc.sync.dma_start(out=q_raw[0][:], in_=q_rows[0])
-        nc.sync.dma_start(out=q_raw[1][:], in_=q_rows[1])
+        q_rows = qT[0].rearrange("(o p j) (h w) -> h o p j w", o=PASSES, j=PACK, h=2)
+        q_raw = {}
+        for h in range(2):
+            for o in range(PASSES):
+                q_raw[h, o] = sb.tile([P, PACK, P], F32, name=f"q_raw{h}{o}", align_bytes=64)
+                nc.sync.dma_start(out=q_raw[h, o][:], in_=q_rows[h, o])
 
         k_scale = sb.tile([P, PASSES * N], U8, name="k_scale", align_bytes=64)
         nc.vector.memset(k_scale[:].bitcast(I32), 0)
@@ -72,40 +74,53 @@ def tile_attend_splade_topk_kernel(tc, qT, k_words, k_scales, kb, offs, out):
                 in_=scale_rows[96 + 8 * quad : 96 + 8 * quad + 8, :].bitcast(I32),
             )
 
-        bias_row = sb.tile([P, N], F32, name="bias_row", tag="q_bf10", align_bytes=64)
+        bias_row = sb.tile([P, N], F32, name="bias_row", align_bytes=64)
         nc.vector.tensor_copy(bias_row[:], bias_pool[:].indirect(offsets[:]))
-        bias_ps = ps.tile([P, 4, P], F32, name="bias_ps", tag="bank0")
+        bias_ps = ps.tile([P, 4, P], F32, name="bias_ps", tag="bank7")
         for s in range(4):
             nc.tensor.transpose(bias_ps[:, s, :], bias_row[:, s * P : (s + 1) * P], ident[:])
-        bias_col = sb.tile([P, 4], F32, name="bias_col")
-        nc.scalar.copy(out=bias_col[:], in_=bias_ps[:, :, P - 1])
 
         pairs = sb.tile([P, N], U32, name="pairs", tag="bias_then_pairs", align_bytes=64)
-        nc.vector.tensor_copy(pairs[:], word_pool[:].indirect(offsets[:]))
+        for g in range(2):
+            columns = slice(g * HALF // 16, (g + 1) * HALF // 16)
+            nc.vector.tensor_copy(pairs[:, g * HALF : (g + 1) * HALF], word_pool[:].indirect(offsets[:, columns]))
         halves = pairs[:].bitcast(U16).rearrange("p (n o) -> p o n", o=PASSES)
 
-        banks = {}
+        k_codes = {}
         q_mx = {}
-        k_codes = []
-        for o in range(PASSES):
-            part = sb.tile([P, 2 * N], U8, name=f"k_codes{o}", tag=("k_low", "q_raw0")[o], align_bytes=64)
-            nc.vector.tensor_copy(out=part[:].bitcast(U16), in_=halves[:, o, :])
-            k_codes.append(part)
-            for h in range(2):
-                grouped = sb.tile([P, P, PACK], BF16, name=f"q_bf{o}{h}", tag=f"q_bf{o}{h}", align_bytes=64)
-                nc.scalar.copy(
-                    out=grouped[:].rearrange("p (c i) t -> p c t i", i=4),
-                    in_=q_raw[o][:, :, h * P : (h + 1) * P].rearrange("p t (c i) -> p c t i", i=4),
-                )
-                codes = sb.tile([P, P], U32, name=f"q_codes{o}{h}", align_bytes=64)
-                plane = sb.tile([P, P], U8, name=f"q_scale{o}{h}", align_bytes=64)
-                nc.vector.quantize_mx(out=codes[:].bitcast(FP8X4), scales=plane[:], in_=grouped[:].rearrange("p w t -> p (w t)"))
-                q_mx[o, h] = codes, plane
 
+        def part_words(o, pieces, tag):
+            k_codes[o] = sb.tile([P, 2 * N], U8, name=f"k_codes{o}", tag=tag, align_bytes=64)
+            width = N // pieces
+            for g in range(pieces):
+                slots = slice(g * width, (g + 1) * width)
+                nc.vector.tensor_copy(out=k_codes[o][:].bitcast(U16)[:, slots], in_=halves[:, o, slots])
+
+        def quantise(h, o, copy):
+            grouped = sb.tile([P, P, PACK], BF16, name=f"q_bf{h}{o}", tag="scales_then_q" if (h, o) == (0, 0) else f"q_bf{h}{o}", align_bytes=64)
+            copy(
+                out=grouped[:].rearrange("p (c i) t -> p c t i", i=4),
+                in_=q_raw[h, o][:].rearrange("p t (c i) -> p c t i", i=4),
+            )
+            codes = sb.tile([P, P], U32, name=f"q_codes{h}{o}", align_bytes=64)
+            plane = sb.tile([P, P], U8, name=f"q_scale{h}{o}", align_bytes=64)
+            nc.vector.quantize_mx(out=codes[:].bitcast(FP8X4), scales=plane[:], in_=grouped[:].rearrange("p w t -> p (w t)"))
+            q_mx[h, o] = codes, plane
+
+        part_words(0, 2, "k_low")
+        quantise(0, 0, nc.scalar.copy)
+        part_words(1, 1, "scales_then_q")
+        quantise(0, 1, nc.scalar.copy)
+        bias_col = sb.tile([P, 4], F32, name="bias_col")
+        nc.vector.tensor_copy(out=bias_col[:], in_=bias_ps[:, :, P - 1])
+        quantise(1, 0, nc.scalar.copy)
+        quantise(1, 1, nc.vector.tensor_copy)
+
+        banks = {}
         acts = {}
-        for o in range(PASSES):
-            for h in range(2):
-                codes, plane = q_mx[o, h]
+        for h in range(2):
+            for o in range(PASSES):
+                codes, plane = q_mx[h, o]
                 for s in range(4):
                     if o == 0:
                         banks[s, h] = ps.tile([P, P], F32, name=f"score{s}{h}", tag=f"bank{4 * h + s}")
@@ -120,7 +135,7 @@ def tile_attend_splade_topk_kernel(tc, qT, k_words, k_scales, kb, offs, out):
                     )
                     if o == 1:
                         act = sb.tile([P, P], F32, name=f"act{s}{h}")
-                        if h == 1 and s % 2 == 0:
+                        if h == 1 and s % 2 == 1:
                             nc.vector.tensor_scalar(act[:], banks[s, h][:], bias_col[:, s : s + 1], 0.0, ALU.add, ALU.max)
                         else:
                             nc.scalar.activation(act[:], banks[s, h][:], ACT.Relu, bias=bias_col[:, s : s + 1])

@@ -32,6 +32,7 @@ def tile_attend_splade_topk_kernel(tc, qT, k_words, k_scales, kb, offs, out):
     nc = tc.nc
     with ExitStack() as ctx:
         sb = ctx.enter_context(tc.tile_pool(name="sb", bufs=1))
+        reused = ctx.enter_context(tc.tile_pool(name="reused", bufs=1))
         ps = ctx.enter_context(tc.psum_pool(name="ps", bufs=1))
 
         ident = sb.tile([P, P], F32, name="ident")
@@ -45,7 +46,7 @@ def tile_attend_splade_topk_kernel(tc, qT, k_words, k_scales, kb, offs, out):
         nc.sync.dma_start(offsets[:], offs)
 
         scale_pool = sb.tile([P, T], U8, name="scale_pool", tag="scales_then_q", align_bytes=64)
-        nc.scalar.dma_start(
+        nc.sync.dma_start(
             out=scale_pool[96:P, :].bitcast(I32),
             in_=k_scales.bitcast(I32).rearrange("o f t -> f o t"),
         )
@@ -53,28 +54,33 @@ def tile_attend_splade_topk_kernel(tc, qT, k_words, k_scales, kb, offs, out):
 
         bias_pool = sb.tile([P, T], F32, name="bias_pool", tag="bias_then_pairs", align_bytes=64)
         nc.sync.dma_start(out=bias_pool[P - 1 : P, :], in_=kb[0:1, :])
-        nc.vector.memset(bias_pool[0 : P - 1, :].bitcast(I32), 0)
+        nc.vector.memset(bias_pool[0 : P - 1, 0:512].bitcast(I32), 0)
+        nc.gpsimd.memset(bias_pool[0 : P - 1, 512:T].bitcast(I32), 0)
 
         word_pool = sb.tile([P, T], U32, name="word_pool")
         nc.sync.dma_start(out=word_pool[:].bitcast(I32), in_=k_words[0].rearrange("p t b -> p (t b)").bitcast(I32))
         q_rows = qT[0].rearrange("(o p j) (h w) -> h o p j w", o=PASSES, j=PACK, h=2)
         q_raw = {}
-        for h in range(2):
-            for o in range(PASSES):
-                q_raw[h, o] = sb.tile([P, PACK, P], F32, name=f"q_raw{h}{o}", align_bytes=64)
-                nc.sync.dma_start(out=q_raw[h, o][:], in_=q_rows[h, o])
+
+        def load_queries(h, o, tag):
+            q_raw[h, o] = sb.tile([P, PACK, P], F32, name=f"q_raw{h}{o}", tag=tag, align_bytes=64)
+            nc.sync.dma_start(out=q_raw[h, o][:], in_=q_rows[h, o])
+
+        for h, o in ((0, 0), (0, 1), (1, 0)):
+            load_queries(h, o, f"q_raw{h}{o}")
 
         k_scale = sb.tile([P, PASSES * N], U8, name="k_scale", align_bytes=64)
         nc.vector.memset(k_scale[:].bitcast(I32), 0)
         scale_rows = sb.tile([P, N], U8, name="scale_rows", align_bytes=64)
         nc.vector.tensor_copy(scale_rows[:], scale_pool[:].indirect(offsets[:]))
         for quad in range(4):
-            nc.scalar.dma_start(
+            nc.sync.dma_start(
                 out=k_scale[32 * quad : 32 * quad + 4, :].bitcast(I32),
                 in_=scale_rows[96 + 8 * quad : 96 + 8 * quad + 8, :].bitcast(I32),
             )
+        load_queries(1, 1, "scales_then_q")
 
-        bias_row = sb.tile([P, N], F32, name="bias_row", align_bytes=64)
+        bias_row = reused.tile([P, N], F32, name="bias_row", align_bytes=64, offset=0)
         nc.vector.tensor_copy(bias_row[:], bias_pool[:].indirect(offsets[:]))
         bias_ps = ps.tile([P, 4, P], F32, name="bias_ps", tag="bank7")
         for s in range(4):
@@ -84,77 +90,109 @@ def tile_attend_splade_topk_kernel(tc, qT, k_words, k_scales, kb, offs, out):
         for g in range(2):
             columns = slice(g * HALF // 16, (g + 1) * HALF // 16)
             nc.vector.tensor_copy(pairs[:, g * HALF : (g + 1) * HALF], word_pool[:].indirect(offsets[:, columns]))
+        bias_col = sb.tile([P, 4], F32, name="bias_col", tag="bias_col")
+        nc.vector.tensor_copy(out=bias_col[:], in_=bias_ps[:, :, P - 1])
         halves = pairs[:].bitcast(U16).rearrange("p (n o) -> p o n", o=PASSES)
 
         k_codes = {}
         q_mx = {}
 
-        def part_words(o, pieces, tag):
-            k_codes[o] = sb.tile([P, 2 * N], U8, name=f"k_codes{o}", tag=tag, align_bytes=64)
+        def part_words(o, pieces, tile):
+            k_codes[o] = tile
             width = N // pieces
             for g in range(pieces):
                 slots = slice(g * width, (g + 1) * width)
                 nc.vector.tensor_copy(out=k_codes[o][:].bitcast(U16)[:, slots], in_=halves[:, o, slots])
 
         def quantise(h, o, copy):
-            grouped = sb.tile([P, P, PACK], BF16, name=f"q_bf{h}{o}", tag="scales_then_q" if (h, o) == (0, 0) else f"q_bf{h}{o}", align_bytes=64)
+            if (h, o) == (1, 1):
+                grouped = reused.tile([P, P, PACK], BF16, name="q_bf11", align_bytes=64, offset=3 * N)
+            else:
+                grouped = sb.tile([P, P, PACK], BF16, name=f"q_bf{h}{o}", tag=f"q_bf{h}{o}", align_bytes=64)
             copy(
                 out=grouped[:].rearrange("p (c i) t -> p c t i", i=4),
                 in_=q_raw[h, o][:].rearrange("p t (c i) -> p c t i", i=4),
             )
             codes = sb.tile([P, P], U32, name=f"q_codes{h}{o}", align_bytes=64)
-            plane = sb.tile([P, P], U8, name=f"q_scale{h}{o}", align_bytes=64)
+            plane = reused.tile([P, P], U8, name=f"q_scale{h}{o}", align_bytes=64, offset=2 * N + (2 * h + o) * P)
             nc.vector.quantize_mx(out=codes[:].bitcast(FP8X4), scales=plane[:], in_=grouped[:].rearrange("p w t -> p (w t)"))
             q_mx[h, o] = codes, plane
 
-        part_words(0, 2, "k_low")
+        part_words(0, 2, reused.tile([P, 2 * N], U8, name="k_low", align_bytes=64, offset=0))
         quantise(0, 0, nc.scalar.copy)
-        part_words(1, 1, "scales_then_q")
+        part_words(1, 1, sb.tile([P, 2 * N], U8, name="k_high", tag="q_bf00", align_bytes=64))
         quantise(0, 1, nc.scalar.copy)
-        bias_col = sb.tile([P, 4], F32, name="bias_col")
-        nc.vector.tensor_copy(out=bias_col[:], in_=bias_ps[:, :, P - 1])
         quantise(1, 0, nc.scalar.copy)
         quantise(1, 1, nc.vector.tensor_copy)
 
+        spread_ps = ps.tile([P, N], F32, name="spread_ps", tag="bank6")
+        for s in range(4):
+            nc.tensor.transpose(spread_ps[:, s * P : (s + 1) * P], bias_col[:, s : s + 1].to_broadcast([P, P]), ident[:])
+        spread = sb.tile([P, N], F32, name="spread", align_bytes=64)
+        nc.scalar.copy(out=spread[:], in_=spread_ps[:])
+
+        rows = ps.tile([P, N], F32, name="rows", tag="bank7")
+        for o in range(PASSES):
+            codes, plane = q_mx[0, o]
+            nc.tensor.matmul_mx(
+                out=rows[:],
+                lhsT=codes[:].bitcast(FP8X4),
+                lhsT_scale=plane[:],
+                rhs=k_codes[o][:].bitcast(FP4X4),
+                rhs_scale=k_scale[:, o * N : (o + 1) * N],
+                start=(o == 0),
+                stop=(o == 1),
+            )
+        biased = reused.tile([P, N], F32, name="biased", align_bytes=64, offset=4 * N)
+        best0 = sb.tile([P, N // SEG], F32, name="best0")
+        for g in range(2):
+            slots = slice(g * HALF, (g + 1) * HALF)
+            nc.vector.tensor_tensor(biased[:, slots], rows[:, slots], spread[:, slots], ALU.add)
+        for g in range(2):
+            nc.vector.tensor_reduce(
+                out=best0[:, g * HALF // SEG : (g + 1) * HALF // SEG],
+                in_=biased[:, g * HALF : (g + 1) * HALF].rearrange("p (j e) -> p j e", e=SEG),
+                axis=mybir.AxisListType.X,
+                op=ALU.max,
+            )
+
         banks = {}
         acts = {}
-        for h in range(2):
-            for o in range(PASSES):
-                codes, plane = q_mx[h, o]
-                for s in range(4):
-                    if o == 0:
-                        banks[s, h] = ps.tile([P, P], F32, name=f"score{s}{h}", tag=f"bank{4 * h + s}")
-                    nc.tensor.matmul_mx(
-                        out=banks[s, h][:],
-                        lhsT=k_codes[o][:, 2 * P * s : 2 * P * (s + 1)].bitcast(FP4X4),
-                        lhsT_scale=k_scale[:, o * N + s * P : o * N + (s + 1) * P],
-                        rhs=codes[:].bitcast(FP8X4),
-                        rhs_scale=plane[:],
-                        start=(o == 0),
-                        stop=(o == 1),
-                    )
-                    if o == 1:
-                        act = sb.tile([P, P], F32, name=f"act{s}{h}")
-                        if h == 1 and s % 2 == 1:
-                            nc.vector.tensor_scalar(act[:], banks[s, h][:], bias_col[:, s : s + 1], 0.0, ALU.add, ALU.max)
-                        else:
-                            nc.scalar.activation(act[:], banks[s, h][:], ACT.Relu, bias=bias_col[:, s : s + 1])
-                        acts[s, h] = act
-
-        for h in range(2):
-            best = sb.tile([P, N // SEG], F32, name=f"best{h}")
-            groups = ((0, 1, 2, 3),) if h == 0 else ((0, 1), (2, 3))
-            for group in groups:
-                turned = ps.tile([P, len(group) * P], F32, name=f"turned{h}{group[0]}", tag=f"bank{h + group[0] // 2}")
-                for i, s in enumerate(group):
-                    nc.tensor.transpose(turned[:, i * P : (i + 1) * P], acts[s, h][:], ident[:])
-                j0 = group[0] * (P // SEG)
-                nc.vector.tensor_reduce(
-                    out=best[:, j0 : j0 + len(group) * (P // SEG)],
-                    in_=turned[:].rearrange("p (j e) -> p j e", e=SEG),
-                    axis=mybir.AxisListType.X,
-                    op=ALU.max,
+        for o in range(PASSES):
+            codes, plane = q_mx[1, o]
+            for s in range(4):
+                if o == 0:
+                    banks[s] = ps.tile([P, P], F32, name=f"score{s}", tag=f"bank{1 + s}")
+                nc.tensor.matmul_mx(
+                    out=banks[s][:],
+                    lhsT=k_codes[o][:, 2 * P * s : 2 * P * (s + 1)].bitcast(FP4X4),
+                    lhsT_scale=k_scale[:, o * N + s * P : o * N + (s + 1) * P],
+                    rhs=codes[:].bitcast(FP8X4),
+                    rhs_scale=plane[:],
+                    start=(o == 0),
+                    stop=(o == 1),
                 )
-            result = sb.tile([P, N // SEG], F32, name=f"result{h}")
-            nc.scalar.activation(result[:], best[:], ACT.Ln, bias=1.0)
-            nc.sync.dma_start(out=out[0, h * P : (h + 1) * P, :], in_=result[:])
+                if o == 1:
+                    acts[s] = sb.tile([P, P], F32, name=f"act{s}")
+                    nc.scalar.activation(acts[s][:], banks[s][:], ACT.Relu, bias=bias_col[:, s : s + 1])
+
+        clipped = sb.tile([P, N // SEG], F32, name="clipped", tag="bias_col")
+        nc.scalar.activation(clipped[:], best0[:], ACT.Relu)
+        result0 = sb.tile([P, N // SEG], F32, name="result0")
+        nc.scalar.activation(result0[:], clipped[:], ACT.Ln, bias=1.0)
+        nc.sync.dma_start(out=out[0, 0:P, :], in_=result0[:])
+
+        best1 = reused.tile([P, N // SEG], F32, name="best1", align_bytes=64, offset=7 * N)
+        for g in range(2):
+            turned = ps.tile([P, HALF], F32, name=f"turned{g}", tag=f"bank{5 + g}")
+            for i in range(2):
+                nc.tensor.transpose(turned[:, i * P : (i + 1) * P], acts[2 * g + i][:], ident[:])
+            nc.vector.tensor_reduce(
+                out=best1[:, g * HALF // SEG : (g + 1) * HALF // SEG],
+                in_=turned[:].rearrange("p (j e) -> p j e", e=SEG),
+                axis=mybir.AxisListType.X,
+                op=ALU.max,
+            )
+        result1 = sb.tile([P, N // SEG], F32, name="result1")
+        nc.scalar.activation(result1[:], best1[:], ACT.Ln, bias=1.0)
+        nc.sync.dma_start(out=out[0, P : 2 * P, :], in_=result1[:])

@@ -32,7 +32,10 @@ def tile_attend_splade_topk_kernel(tc, qT, k_words, k_scales, kb, offs, out):
     nc = tc.nc
     with ExitStack() as ctx:
         sb = ctx.enter_context(tc.tile_pool(name="sb", bufs=1))
-        reused = ctx.enter_context(tc.tile_pool(name="reused", bufs=1))
+        on_bias_pool = ctx.enter_context(tc.tile_pool(name="on_bias_pool", bufs=1))
+        on_bias_row = ctx.enter_context(tc.tile_pool(name="on_bias_row", bufs=1))
+        on_first_q = ctx.enter_context(tc.tile_pool(name="on_first_q", bufs=1))
+        on_scale_pool = ctx.enter_context(tc.tile_pool(name="on_scale_pool", bufs=1))
         ps = ctx.enter_context(tc.psum_pool(name="ps", bufs=1))
 
         ident = sb.tile([P, P], F32, name="ident")
@@ -45,95 +48,119 @@ def tile_attend_splade_topk_kernel(tc, qT, k_words, k_scales, kb, offs, out):
         offsets = sb.tile([P, N // 16], U16, name="offsets")
         nc.sync.dma_start(offsets[:], offs)
 
-        scale_pool = sb.tile([P, T], U8, name="scale_pool", tag="scales_then_q", align_bytes=64)
+        scale_pool = on_scale_pool.tile([P, T], U8, name="scale_pool", align_bytes=64, offset=0)
         nc.sync.dma_start(
             out=scale_pool[96:P, :].bitcast(I32),
             in_=k_scales.bitcast(I32).rearrange("o f t -> f o t"),
         )
         nc.vector.memset(scale_pool[0:96, :].bitcast(I32), 0)
 
-        bias_pool = sb.tile([P, T], F32, name="bias_pool", tag="bias_then_pairs", align_bytes=64)
+        bias_pool = on_bias_pool.tile([P, T], F32, name="bias_pool", align_bytes=64, offset=0)
         nc.sync.dma_start(out=bias_pool[P - 1 : P, :], in_=kb[0:1, :])
-        nc.vector.memset(bias_pool[0 : P - 1, 0:512].bitcast(I32), 0)
-        nc.gpsimd.memset(bias_pool[0 : P - 1, 512:T].bitcast(I32), 0)
+        nc.vector.memset(bias_pool[0 : P - 1, 0:1280].bitcast(I32), 0)
+        nc.gpsimd.memset(bias_pool[0 : P - 1, 1280:T].bitcast(I32), 0)
 
         word_pool = sb.tile([P, T], U32, name="word_pool")
         nc.sync.dma_start(out=word_pool[:].bitcast(I32), in_=k_words[0].rearrange("p t b -> p (t b)").bitcast(I32))
         q_rows = qT[0].rearrange("(o p j) (h w) -> h o p j w", o=PASSES, j=PACK, h=2)
-        q_raw = {}
-
-        def load_queries(h, o, tag):
-            q_raw[h, o] = sb.tile([P, PACK, P], F32, name=f"q_raw{h}{o}", tag=tag, align_bytes=64)
+        q_raw = {
+            (0, 0): on_first_q.tile([P, PACK, P], F32, name="q_raw00", align_bytes=64, offset=0),
+            (1, 0): sb.tile([P, PACK, P], F32, name="q_raw10", align_bytes=64),
+            (1, 1): sb.tile([P, PACK, P], F32, name="q_raw11", align_bytes=64),
+        }
+        for h, o in ((0, 0), (1, 0), (1, 1)):
             nc.sync.dma_start(out=q_raw[h, o][:], in_=q_rows[h, o])
-
-        for h, o in ((0, 0), (0, 1), (1, 0)):
-            load_queries(h, o, f"q_raw{h}{o}")
 
         k_scale = sb.tile([P, PASSES * N], U8, name="k_scale", align_bytes=64)
         nc.vector.memset(k_scale[:].bitcast(I32), 0)
         scale_rows = sb.tile([P, N], U8, name="scale_rows", align_bytes=64)
         nc.vector.tensor_copy(scale_rows[:], scale_pool[:].indirect(offsets[:]))
         for quad in range(4):
-            nc.sync.dma_start(
+            (nc.sync, nc.scalar)[quad % 2].dma_start(
                 out=k_scale[32 * quad : 32 * quad + 4, :].bitcast(I32),
                 in_=scale_rows[96 + 8 * quad : 96 + 8 * quad + 8, :].bitcast(I32),
             )
-        load_queries(1, 1, "scales_then_q")
+        q_raw[0, 1] = on_scale_pool.tile([P, PACK, P], F32, name="q_raw01", align_bytes=64, offset=0)
+        nc.sync.dma_start(out=q_raw[0, 1][:], in_=q_rows[0, 1])
 
-        bias_row = reused.tile([P, N], F32, name="bias_row", align_bytes=64, offset=0)
-        nc.vector.tensor_copy(bias_row[:], bias_pool[:].indirect(offsets[:]))
+        def gather_half(dest, window, g):
+            columns = slice(g * HALF // 16, (g + 1) * HALF // 16)
+            nc.vector.tensor_copy(dest[:, g * HALF : (g + 1) * HALF], window[:].indirect(offsets[:, columns]))
+
+        bias_row = on_bias_row.tile([P, N], F32, name="bias_row", align_bytes=64, offset=0)
         bias_ps = ps.tile([P, 4, P], F32, name="bias_ps", tag="bank7")
+        for g in range(2):
+            gather_half(bias_row, bias_pool, g)
         for s in range(4):
             nc.tensor.transpose(bias_ps[:, s, :], bias_row[:, s * P : (s + 1) * P], ident[:])
 
-        pairs = sb.tile([P, N], U32, name="pairs", tag="bias_then_pairs", align_bytes=64)
+        pairs = on_bias_pool.tile([P, N], U32, name="pairs", align_bytes=64, offset=8 * N)
         for g in range(2):
-            columns = slice(g * HALF // 16, (g + 1) * HALF // 16)
-            nc.vector.tensor_copy(pairs[:, g * HALF : (g + 1) * HALF], word_pool[:].indirect(offsets[:, columns]))
-        bias_col = sb.tile([P, 4], F32, name="bias_col", tag="bias_col")
-        nc.vector.tensor_copy(out=bias_col[:], in_=bias_ps[:, :, P - 1])
+            gather_half(pairs, word_pool, g)
         halves = pairs[:].bitcast(U16).rearrange("p (n o) -> p o n", o=PASSES)
 
-        k_codes = {}
+        k_codes = [on_first_q.tile([P, 2 * N], U8, name=f"k_codes{o}", align_bytes=64, offset=o * 2 * N) for o in range(PASSES)]
+        q_bf = {
+            (0, 0): on_bias_pool.tile([P, P, PACK], BF16, name="q_bf00", align_bytes=64, offset=0),
+            (1, 0): on_bias_row.tile([P, P, PACK], BF16, name="q_bf10", align_bytes=64, offset=0),
+            (1, 1): on_bias_row.tile([P, P, PACK], BF16, name="q_bf11", align_bytes=64, offset=2 * N),
+            (0, 1): sb.tile([P, P, PACK], BF16, name="q_bf01", align_bytes=64),
+        }
         q_mx = {}
 
-        def part_words(o, pieces, tile):
-            k_codes[o] = tile
-            width = N // pieces
-            for g in range(pieces):
-                slots = slice(g * width, (g + 1) * width)
-                nc.vector.tensor_copy(out=k_codes[o][:].bitcast(U16)[:, slots], in_=halves[:, o, slots])
+        def part_words(o, slots):
+            nc.vector.tensor_copy(out=k_codes[o][:].bitcast(U16)[:, slots], in_=halves[:, o, slots])
 
         def quantise(h, o, copy):
-            if (h, o) == (1, 1):
-                grouped = reused.tile([P, P, PACK], BF16, name="q_bf11", align_bytes=64, offset=3 * N)
-            else:
-                grouped = sb.tile([P, P, PACK], BF16, name=f"q_bf{h}{o}", tag=f"q_bf{h}{o}", align_bytes=64)
+            grouped = q_bf[h, o]
             copy(
                 out=grouped[:].rearrange("p (c i) t -> p c t i", i=4),
                 in_=q_raw[h, o][:].rearrange("p t (c i) -> p c t i", i=4),
             )
             codes = sb.tile([P, P], U32, name=f"q_codes{h}{o}", align_bytes=64)
-            plane = reused.tile([P, P], U8, name=f"q_scale{h}{o}", align_bytes=64, offset=2 * N + (2 * h + o) * P)
+            plane = sb.tile([P, P], U8, name=f"q_scale{h}{o}", align_bytes=64)
             nc.vector.quantize_mx(out=codes[:].bitcast(FP8X4), scales=plane[:], in_=grouped[:].rearrange("p w t -> p (w t)"))
             q_mx[h, o] = codes, plane
 
-        part_words(0, 2, reused.tile([P, 2 * N], U8, name="k_low", align_bytes=64, offset=0))
         quantise(0, 0, nc.scalar.copy)
-        part_words(1, 1, sb.tile([P, 2 * N], U8, name="k_high", tag="q_bf00", align_bytes=64))
-        quantise(0, 1, nc.scalar.copy)
+        bias_col = sb.tile([P, 4], F32, name="bias_col", tag="bias_col")
+        nc.scalar.copy(out=bias_col[:], in_=bias_ps[:, :, P - 1])
+        part_words(0, slice(0, HALF))
+        part_words(0, slice(HALF, N))
         quantise(1, 0, nc.scalar.copy)
-        quantise(1, 1, nc.vector.tensor_copy)
+        part_words(1, slice(0, N))
+        quantise(1, 1, nc.scalar.copy)
+        quantise(0, 1, nc.vector.tensor_copy)
 
-        spread_ps = ps.tile([P, N], F32, name="spread_ps", tag="bank6")
-        for s in range(4):
-            nc.tensor.transpose(spread_ps[:, s * P : (s + 1) * P], bias_col[:, s : s + 1].to_broadcast([P, P]), ident[:])
         spread = sb.tile([P, N], F32, name="spread", align_bytes=64)
-        nc.scalar.copy(out=spread[:], in_=spread_ps[:])
+        for g in range(2):
+            spread_ps = ps.tile([P, HALF], F32, name=f"spread_ps{g}", tag=f"bank{2 + g}")
+            for i in range(2):
+                s = 2 * g + i
+                nc.tensor.transpose(spread_ps[:, i * P : (i + 1) * P], bias_col[:, s : s + 1].to_broadcast([P, P]), ident[:])
+            nc.scalar.copy(out=spread[:, g * HALF : (g + 1) * HALF], in_=spread_ps[:])
 
-        rows = ps.tile([P, N], F32, name="rows", tag="bank7")
-        for o in range(PASSES):
+        banks = {}
+
+        def slots_by_queries(s, o):
             codes, plane = q_mx[0, o]
+            if o == 0:
+                banks[s] = ps.tile([P, P], F32, name=f"score{s}", tag=f"bank{(7, 1, 2, 3)[s]}")
+            nc.tensor.matmul_mx(
+                out=banks[s][:],
+                lhsT=k_codes[o][:, 2 * P * s : 2 * P * (s + 1)].bitcast(FP4X4),
+                lhsT_scale=k_scale[:, o * N + s * P : o * N + (s + 1) * P],
+                rhs=codes[:].bitcast(FP8X4),
+                rhs_scale=plane[:],
+                start=(o == 0),
+                stop=(o == 1),
+            )
+
+        for s in (0, 1):
+            slots_by_queries(s, 0)
+        rows = ps.tile([P, N], F32, name="rows", tag="bank0")
+        for o in range(PASSES):
+            codes, plane = q_mx[1, o]
             nc.tensor.matmul_mx(
                 out=rows[:],
                 lhsT=codes[:].bitcast(FP8X4),
@@ -143,56 +170,45 @@ def tile_attend_splade_topk_kernel(tc, qT, k_words, k_scales, kb, offs, out):
                 start=(o == 0),
                 stop=(o == 1),
             )
-        biased = reused.tile([P, N], F32, name="biased", align_bytes=64, offset=4 * N)
-        best0 = sb.tile([P, N // SEG], F32, name="best0")
+        for s in (2, 3):
+            slots_by_queries(s, 0)
+
+        biased = on_scale_pool.tile([P, N], F32, name="biased", align_bytes=64, offset=0)
+        best_rows = sb.tile([P, N // SEG], F32, name="best_rows")
         for g in range(2):
             slots = slice(g * HALF, (g + 1) * HALF)
             nc.vector.tensor_tensor(biased[:, slots], rows[:, slots], spread[:, slots], ALU.add)
         for g in range(2):
             nc.vector.tensor_reduce(
-                out=best0[:, g * HALF // SEG : (g + 1) * HALF // SEG],
+                out=best_rows[:, g * HALF // SEG : (g + 1) * HALF // SEG],
                 in_=biased[:, g * HALF : (g + 1) * HALF].rearrange("p (j e) -> p j e", e=SEG),
                 axis=mybir.AxisListType.X,
                 op=ALU.max,
             )
 
-        banks = {}
         acts = {}
-        for o in range(PASSES):
-            codes, plane = q_mx[1, o]
-            for s in range(4):
-                if o == 0:
-                    banks[s] = ps.tile([P, P], F32, name=f"score{s}", tag=f"bank{1 + s}")
-                nc.tensor.matmul_mx(
-                    out=banks[s][:],
-                    lhsT=k_codes[o][:, 2 * P * s : 2 * P * (s + 1)].bitcast(FP4X4),
-                    lhsT_scale=k_scale[:, o * N + s * P : o * N + (s + 1) * P],
-                    rhs=codes[:].bitcast(FP8X4),
-                    rhs_scale=plane[:],
-                    start=(o == 0),
-                    stop=(o == 1),
-                )
-                if o == 1:
-                    acts[s] = sb.tile([P, P], F32, name=f"act{s}")
-                    nc.scalar.activation(acts[s][:], banks[s][:], ACT.Relu, bias=bias_col[:, s : s + 1])
+        for s in range(4):
+            slots_by_queries(s, 1)
+            acts[s] = sb.tile([P, P], F32, name=f"act{s}")
+            nc.scalar.activation(acts[s][:], banks[s][:], ACT.Relu, bias=bias_col[:, s : s + 1])
 
         clipped = sb.tile([P, N // SEG], F32, name="clipped", tag="bias_col")
-        nc.scalar.activation(clipped[:], best0[:], ACT.Relu)
-        result0 = sb.tile([P, N // SEG], F32, name="result0")
-        nc.scalar.activation(result0[:], clipped[:], ACT.Ln, bias=1.0)
-        nc.sync.dma_start(out=out[0, 0:P, :], in_=result0[:])
+        nc.scalar.activation(clipped[:], best_rows[:], ACT.Relu)
+        result_rows = sb.tile([P, N // SEG], F32, name="result_rows")
+        nc.scalar.activation(result_rows[:], clipped[:], ACT.Ln, bias=1.0)
+        nc.sync.dma_start(out=out[0, P : 2 * P, :], in_=result_rows[:])
 
-        best1 = reused.tile([P, N // SEG], F32, name="best1", align_bytes=64, offset=7 * N)
-        for g in range(2):
-            turned = ps.tile([P, HALF], F32, name=f"turned{g}", tag=f"bank{5 + g}")
-            for i in range(2):
-                nc.tensor.transpose(turned[:, i * P : (i + 1) * P], acts[2 * g + i][:], ident[:])
+        best = on_scale_pool.tile([P, N // SEG], F32, name="best", align_bytes=64, offset=3 * N)
+        for first, count, bank in ((0, 2, 4), (2, 1, 5), (3, 1, 6)):
+            turned = ps.tile([P, count * P], F32, name=f"turned{first}", tag=f"bank{bank}")
+            for i in range(count):
+                nc.tensor.transpose(turned[:, i * P : (i + 1) * P], acts[first + i][:], ident[:])
             nc.vector.tensor_reduce(
-                out=best1[:, g * HALF // SEG : (g + 1) * HALF // SEG],
+                out=best[:, first * P // SEG : (first + count) * P // SEG],
                 in_=turned[:].rearrange("p (j e) -> p j e", e=SEG),
                 axis=mybir.AxisListType.X,
                 op=ALU.max,
             )
-        result1 = sb.tile([P, N // SEG], F32, name="result1")
-        nc.scalar.activation(result1[:], best1[:], ACT.Ln, bias=1.0)
-        nc.sync.dma_start(out=out[0, P : 2 * P, :], in_=result1[:])
+        result = sb.tile([P, N // SEG], F32, name="result")
+        nc.scalar.activation(result[:], best[:], ACT.Ln, bias=1.0)
+        nc.sync.dma_start(out=out[0, 0:P, :], in_=result[:])

@@ -36,6 +36,7 @@ def tile_attend_splade_topk_kernel(tc, qT, k_words, k_scales, kb, offs, out):
         on_bias_row = ctx.enter_context(tc.tile_pool(name="on_bias_row", bufs=1))
         on_first_q = ctx.enter_context(tc.tile_pool(name="on_first_q", bufs=1))
         on_scale_pool = ctx.enter_context(tc.tile_pool(name="on_scale_pool", bufs=1))
+        on_second_q = ctx.enter_context(tc.tile_pool(name="on_second_q", bufs=1))
         ps = ctx.enter_context(tc.psum_pool(name="ps", bufs=1))
 
         ident = sb.tile([P, P], F32, name="ident")
@@ -65,10 +66,10 @@ def tile_attend_splade_topk_kernel(tc, qT, k_words, k_scales, kb, offs, out):
         q_rows = qT[0].rearrange("(o p j) (h w) -> h o p j w", o=PASSES, j=PACK, h=2)
         q_raw = {
             (0, 0): on_first_q.tile([P, PACK, P], F32, name="q_raw00", align_bytes=64, offset=0),
+            (0, 1): on_second_q.tile([P, PACK, P], F32, name="q_raw01", align_bytes=64, offset=0),
             (1, 0): sb.tile([P, PACK, P], F32, name="q_raw10", align_bytes=64),
-            (1, 1): sb.tile([P, PACK, P], F32, name="q_raw11", align_bytes=64),
         }
-        for h, o in ((0, 0), (1, 0), (1, 1)):
+        for h, o in ((0, 0), (0, 1), (1, 0)):
             nc.sync.dma_start(out=q_raw[h, o][:], in_=q_rows[h, o])
 
         k_scale = sb.tile([P, PASSES * N], U8, name="k_scale", align_bytes=64)
@@ -80,8 +81,8 @@ def tile_attend_splade_topk_kernel(tc, qT, k_words, k_scales, kb, offs, out):
                 out=k_scale[32 * quad : 32 * quad + 4, :].bitcast(I32),
                 in_=scale_rows[96 + 8 * quad : 96 + 8 * quad + 8, :].bitcast(I32),
             )
-        q_raw[0, 1] = on_scale_pool.tile([P, PACK, P], F32, name="q_raw01", align_bytes=64, offset=0)
-        nc.sync.dma_start(out=q_raw[0, 1][:], in_=q_rows[0, 1])
+        q_raw[1, 1] = on_scale_pool.tile([P, PACK, P], F32, name="q_raw11", align_bytes=64, offset=0)
+        nc.sync.dma_start(out=q_raw[1, 1][:], in_=q_rows[1, 1])
 
         def gather_half(dest, window, g):
             columns = slice(g * HALF // 16, (g + 1) * HALF // 16)
@@ -99,85 +100,85 @@ def tile_attend_splade_topk_kernel(tc, qT, k_words, k_scales, kb, offs, out):
             gather_half(pairs, word_pool, g)
         halves = pairs[:].bitcast(U16).rearrange("p (n o) -> p o n", o=PASSES)
 
-        k_codes = [on_first_q.tile([P, 2 * N], U8, name=f"k_codes{o}", align_bytes=64, offset=o * 2 * N) for o in range(PASSES)]
+        k_codes = {
+            (0, 0): on_first_q.tile([P, N], U8, name="k_codes00", align_bytes=64, offset=0),
+            (0, 1): on_first_q.tile([P, N], U8, name="k_codes01", align_bytes=64, offset=N),
+            (1, 0): on_first_q.tile([P, N], U8, name="k_codes10", align_bytes=64, offset=2 * N),
+            (1, 1): on_second_q.tile([P, N], U8, name="k_codes11", align_bytes=64, offset=0),
+        }
         q_bf = {
             (0, 0): on_bias_pool.tile([P, P, PACK], BF16, name="q_bf00", align_bytes=64, offset=0),
-            (1, 0): on_bias_row.tile([P, P, PACK], BF16, name="q_bf10", align_bytes=64, offset=0),
-            (1, 1): on_bias_row.tile([P, P, PACK], BF16, name="q_bf11", align_bytes=64, offset=2 * N),
-            (0, 1): sb.tile([P, P, PACK], BF16, name="q_bf01", align_bytes=64),
+            (0, 1): on_bias_row.tile([P, P, PACK], BF16, name="q_bf01", align_bytes=64, offset=0),
+            (1, 0): on_bias_row.tile([P, P, PACK], BF16, name="q_bf10", align_bytes=64, offset=2 * N),
+            (1, 1): sb.tile([P, P, PACK], BF16, name="q_bf11", align_bytes=64),
         }
         q_mx = {}
 
-        def part_words(o, slots):
-            nc.vector.tensor_copy(out=k_codes[o][:].bitcast(U16)[:, slots], in_=halves[:, o, slots])
+        def part_words(o, g):
+            nc.vector.tensor_copy(out=k_codes[o, g][:].bitcast(U16), in_=halves[:, o, g * HALF : (g + 1) * HALF])
 
-        def quantise(h, o, copy):
-            grouped = q_bf[h, o]
+        def cast(h, o, copy):
             copy(
-                out=grouped[:].rearrange("p (c i) t -> p c t i", i=4),
+                out=q_bf[h, o][:].rearrange("p (c i) t -> p c t i", i=4),
                 in_=q_raw[h, o][:].rearrange("p t (c i) -> p c t i", i=4),
             )
+
+        def quantise(h, o):
             codes = sb.tile([P, P], U32, name=f"q_codes{h}{o}", align_bytes=64)
             plane = sb.tile([P, P], U8, name=f"q_scale{h}{o}", align_bytes=64)
-            nc.vector.quantize_mx(out=codes[:].bitcast(FP8X4), scales=plane[:], in_=grouped[:].rearrange("p w t -> p (w t)"))
-            q_mx[h, o] = codes, plane
+            nc.vector.quantize_mx(out=codes[:].bitcast(FP8X4), scales=plane[:], in_=q_bf[h, o][:].rearrange("p w t -> p (w t)"))
+            q_mx[h, o] = codes[:].bitcast(FP8X4), plane[:]
 
-        quantise(0, 0, nc.scalar.copy)
+        def keys(o, s):
+            return k_codes[o, s // 2][:, 2 * P * (s % 2) : 2 * P * (s % 2 + 1)].bitcast(FP4X4), k_scale[:, o * N + s * P : o * N + (s + 1) * P]
+
+        def product(bank, stationary, moving, o):
+            nc.tensor.matmul_mx(
+                out=bank[:],
+                lhsT=stationary[0],
+                lhsT_scale=stationary[1],
+                rhs=moving[0],
+                rhs_scale=moving[1],
+                start=(o == 0),
+                stop=(o == 1),
+            )
+
+        cast(0, 0, nc.scalar.copy)
+        quantise(0, 0)
         bias_col = sb.tile([P, 4], F32, name="bias_col", tag="bias_col")
         nc.scalar.copy(out=bias_col[:], in_=bias_ps[:, :, P - 1])
-        part_words(0, slice(0, HALF))
-        part_words(0, slice(HALF, N))
-        quantise(1, 0, nc.scalar.copy)
-        part_words(1, slice(0, N))
-        quantise(1, 1, nc.scalar.copy)
-        quantise(0, 1, nc.vector.tensor_copy)
+        part_words(0, 0)
+        part_words(0, 1)
+        part_words(1, 0)
+        cast(0, 1, nc.scalar.copy)
+        quantise(0, 1)
+        part_words(1, 1)
+        cast(1, 0, nc.scalar.copy)
+        quantise(1, 0)
+        cast(1, 1, nc.scalar.copy)
 
-        spread = sb.tile([P, N], F32, name="spread", align_bytes=64)
+        spread = on_scale_pool.tile([P, N], F32, name="spread", align_bytes=64, offset=0)
+        spread_ps = ps.tile([P, N], F32, name="spread_ps", tag="bank5")
+        for s in range(4):
+            nc.tensor.transpose(spread_ps[:, s * P : (s + 1) * P], bias_col[:, s : s + 1].to_broadcast([P, P]), ident[:])
         for g in range(2):
-            spread_ps = ps.tile([P, HALF], F32, name=f"spread_ps{g}", tag=f"bank{2 + g}")
-            for i in range(2):
-                s = 2 * g + i
-                nc.tensor.transpose(spread_ps[:, i * P : (i + 1) * P], bias_col[:, s : s + 1].to_broadcast([P, P]), ident[:])
-            nc.scalar.copy(out=spread[:, g * HALF : (g + 1) * HALF], in_=spread_ps[:])
+            nc.scalar.copy(out=spread[:, g * HALF : (g + 1) * HALF], in_=spread_ps[:, g * HALF : (g + 1) * HALF])
 
-        banks = {}
-
-        def slots_by_queries(s, o):
-            codes, plane = q_mx[0, o]
-            if o == 0:
-                banks[s] = ps.tile([P, P], F32, name=f"score{s}", tag=f"bank{(7, 1, 2, 3)[s]}")
-            nc.tensor.matmul_mx(
-                out=banks[s][:],
-                lhsT=k_codes[o][:, 2 * P * s : 2 * P * (s + 1)].bitcast(FP4X4),
-                lhsT_scale=k_scale[:, o * N + s * P : o * N + (s + 1) * P],
-                rhs=codes[:].bitcast(FP8X4),
-                rhs_scale=plane[:],
-                start=(o == 0),
-                stop=(o == 1),
-            )
-
-        for s in (0, 1):
-            slots_by_queries(s, 0)
-        rows = ps.tile([P, N], F32, name="rows", tag="bank0")
+        by_query = [ps.tile([P, P], F32, name=f"by_query{s}", tag=f"bank{(7, 1, 2, 3)[s]}") for s in range(4)]
         for o in range(PASSES):
-            codes, plane = q_mx[1, o]
-            nc.tensor.matmul_mx(
-                out=rows[:],
-                lhsT=codes[:].bitcast(FP8X4),
-                lhsT_scale=plane[:],
-                rhs=k_codes[o][:].bitcast(FP4X4),
-                rhs_scale=k_scale[:, o * N : (o + 1) * N],
-                start=(o == 0),
-                stop=(o == 1),
-            )
-        for s in (2, 3):
-            slots_by_queries(s, 0)
+            for s in range(4):
+                product(by_query[s], q_mx[0, o], keys(o, s), o)
 
-        biased = on_scale_pool.tile([P, N], F32, name="biased", align_bytes=64, offset=0)
+        biased = sb.tile([P, N], F32, name="biased", tag="biased_then_best", align_bytes=64)
+
+        def add_bias(s):
+            slots = slice(s * P, (s + 1) * P)
+            nc.vector.tensor_tensor(biased[:, slots], by_query[s][:], spread[:, slots], ALU.add)
+
+        quantise(1, 1)
+        for s in range(4):
+            add_bias(s)
         best_rows = sb.tile([P, N // SEG], F32, name="best_rows")
-        for g in range(2):
-            slots = slice(g * HALF, (g + 1) * HALF)
-            nc.vector.tensor_tensor(biased[:, slots], rows[:, slots], spread[:, slots], ALU.add)
         for g in range(2):
             nc.vector.tensor_reduce(
                 out=best_rows[:, g * HALF // SEG : (g + 1) * HALF // SEG],
@@ -186,20 +187,23 @@ def tile_attend_splade_topk_kernel(tc, qT, k_words, k_scales, kb, offs, out):
                 op=ALU.max,
             )
 
+        by_slot = [ps.tile([P, P], F32, name=f"by_slot{s}", tag=f"bank{(0, 6, 4, 5)[s]}") for s in range(4)]
         acts = {}
-        for s in range(4):
-            slots_by_queries(s, 1)
-            acts[s] = sb.tile([P, P], F32, name=f"act{s}")
-            nc.scalar.activation(acts[s][:], banks[s][:], ACT.Relu, bias=bias_col[:, s : s + 1])
+        for o in range(PASSES):
+            for s in range(4):
+                product(by_slot[s], keys(o, s), q_mx[1, o], o)
+                if o == 1:
+                    acts[s] = sb.tile([P, P], F32, name=f"act{s}")
+                    nc.scalar.activation(acts[s][:], by_slot[s][:], ACT.Relu, bias=bias_col[:, s : s + 1])
 
         clipped = sb.tile([P, N // SEG], F32, name="clipped", tag="bias_col")
         nc.scalar.activation(clipped[:], best_rows[:], ACT.Relu)
         result_rows = sb.tile([P, N // SEG], F32, name="result_rows")
         nc.scalar.activation(result_rows[:], clipped[:], ACT.Ln, bias=1.0)
-        nc.sync.dma_start(out=out[0, P : 2 * P, :], in_=result_rows[:])
+        nc.sync.dma_start(out=out[0, 0:P, :], in_=result_rows[:])
 
-        best = on_scale_pool.tile([P, N // SEG], F32, name="best", align_bytes=64, offset=3 * N)
-        for first, count, bank in ((0, 2, 4), (2, 1, 5), (3, 1, 6)):
+        best = sb.tile([P, N // SEG], F32, name="best", tag="biased_then_best", align_bytes=64)
+        for first, count, bank in ((0, 2, 7), (2, 1, 1), (3, 1, 2)):
             turned = ps.tile([P, count * P], F32, name=f"turned{first}", tag=f"bank{bank}")
             for i in range(count):
                 nc.tensor.transpose(turned[:, i * P : (i + 1) * P], acts[first + i][:], ident[:])
@@ -211,4 +215,4 @@ def tile_attend_splade_topk_kernel(tc, qT, k_words, k_scales, kb, offs, out):
             )
         result = sb.tile([P, N // SEG], F32, name="result")
         nc.scalar.activation(result[:], best[:], ACT.Ln, bias=1.0)
-        nc.sync.dma_start(out=out[0, 0:P, :], in_=result[:])
+        nc.sync.dma_start(out=out[0, P : 2 * P, :], in_=result[:])

@@ -37,6 +37,7 @@ def tile_attend_splade_topk_kernel(tc, qT, k_words, k_scales, kb, offs, out):
         on_first_q = ctx.enter_context(tc.tile_pool(name="on_first_q", bufs=1))
         on_scale_pool = ctx.enter_context(tc.tile_pool(name="on_scale_pool", bufs=1))
         on_second_q = ctx.enter_context(tc.tile_pool(name="on_second_q", bufs=1))
+        on_third_q = ctx.enter_context(tc.tile_pool(name="on_third_q", bufs=1))
         ps = ctx.enter_context(tc.psum_pool(name="ps", bufs=1))
 
         ident = sb.tile([P, P], F32, name="ident")
@@ -67,7 +68,7 @@ def tile_attend_splade_topk_kernel(tc, qT, k_words, k_scales, kb, offs, out):
         q_raw = {
             (0, 0): on_first_q.tile([P, PACK, P], F32, name="q_raw00", align_bytes=64, offset=0),
             (0, 1): on_second_q.tile([P, PACK, P], F32, name="q_raw01", align_bytes=64, offset=0),
-            (1, 0): sb.tile([P, PACK, P], F32, name="q_raw10", align_bytes=64),
+            (1, 0): on_third_q.tile([P, PACK, P], F32, name="q_raw10", align_bytes=64, offset=0),
         }
         for h, o in ((0, 0), (0, 1), (1, 0)):
             nc.sync.dma_start(out=q_raw[h, o][:], in_=q_rows[h, o])
@@ -157,23 +158,26 @@ def tile_attend_splade_topk_kernel(tc, qT, k_words, k_scales, kb, offs, out):
         quantise(1, 0)
         cast(1, 1, nc.scalar.copy)
 
-        spread = on_scale_pool.tile([P, N], F32, name="spread", align_bytes=64, offset=0)
+        spread = [
+            on_third_q.tile([P, HALF], F32, name="spread0", align_bytes=64, offset=0),
+            on_scale_pool.tile([P, HALF], F32, name="spread1", align_bytes=64, offset=0),
+        ]
         spread_ps = ps.tile([P, N], F32, name="spread_ps", tag="bank5")
         for s in range(4):
             nc.tensor.transpose(spread_ps[:, s * P : (s + 1) * P], bias_col[:, s : s + 1].to_broadcast([P, P]), ident[:])
-        for g in range(2):
-            nc.scalar.copy(out=spread[:, g * HALF : (g + 1) * HALF], in_=spread_ps[:, g * HALF : (g + 1) * HALF])
+        for g, copy in enumerate((nc.vector.tensor_copy, nc.scalar.copy)):
+            copy(out=spread[g][:], in_=spread_ps[:, g * HALF : (g + 1) * HALF])
 
         by_query = [ps.tile([P, P], F32, name=f"by_query{s}", tag=f"bank{(7, 1, 2, 3)[s]}") for s in range(4)]
         for o in range(PASSES):
             for s in range(4):
                 product(by_query[s], q_mx[0, o], keys(o, s), o)
 
-        biased = sb.tile([P, N], F32, name="biased", tag="biased_then_best", align_bytes=64)
+        biased = on_scale_pool.tile([P, N], F32, name="biased", align_bytes=64, offset=2 * N)
 
         def add_bias(s):
             slots = slice(s * P, (s + 1) * P)
-            nc.vector.tensor_tensor(biased[:, slots], by_query[s][:], spread[:, slots], ALU.add)
+            nc.vector.tensor_tensor(biased[:, slots], by_query[s][:], spread[s // 2][:, (s % 2) * P : (s % 2 + 1) * P], ALU.add)
 
         quantise(1, 1)
         for s in range(4):
@@ -189,12 +193,11 @@ def tile_attend_splade_topk_kernel(tc, qT, k_words, k_scales, kb, offs, out):
 
         by_slot = [ps.tile([P, P], F32, name=f"by_slot{s}", tag=f"bank{(0, 6, 4, 5)[s]}") for s in range(4)]
         acts = {}
-        for o in range(PASSES):
-            for s in range(4):
-                product(by_slot[s], keys(o, s), q_mx[1, o], o)
-                if o == 1:
-                    acts[s] = sb.tile([P, P], F32, name=f"act{s}")
-                    nc.scalar.activation(acts[s][:], by_slot[s][:], ACT.Relu, bias=bias_col[:, s : s + 1])
+        for s, o in ((0, 0), (1, 0), (2, 0), (0, 1), (3, 0), (1, 1), (2, 1), (3, 1)):
+            product(by_slot[s], keys(o, s), q_mx[1, o], o)
+            if o == 1:
+                acts[s] = sb.tile([P, P], F32, name=f"act{s}")
+                nc.scalar.activation(acts[s][:], by_slot[s][:], ACT.Relu, bias=bias_col[:, s : s + 1])
 
         clipped = sb.tile([P, N // SEG], F32, name="clipped", tag="bias_col")
         nc.scalar.activation(clipped[:], best_rows[:], ACT.Relu)
@@ -202,7 +205,7 @@ def tile_attend_splade_topk_kernel(tc, qT, k_words, k_scales, kb, offs, out):
         nc.scalar.activation(result_rows[:], clipped[:], ACT.Ln, bias=1.0)
         nc.sync.dma_start(out=out[0, 0:P, :], in_=result_rows[:])
 
-        best = sb.tile([P, N // SEG], F32, name="best", tag="biased_then_best", align_bytes=64)
+        best = on_scale_pool.tile([P, N // SEG], F32, name="best", align_bytes=64, offset=5 * N)
         for first, count, bank in ((0, 2, 7), (2, 1, 1), (3, 1, 2)):
             turned = ps.tile([P, count * P], F32, name=f"turned{first}", tag=f"bank{bank}")
             for i in range(count):

@@ -23,6 +23,7 @@ N = 512
 T = 2048
 SEG = 8
 HALF = N // 2
+RUNS = N // SEG
 
 FLOPS = 2 * NQ * N * D
 BYTES = D * NQ * 4 + P * T * 4 + PASSES * 16 * T + T * 4 + P * (N // 16) * 2 + NQ * (N // SEG) * 4
@@ -34,10 +35,9 @@ def tile_attend_splade_topk_kernel(tc, qT, k_words, k_scales, kb, offs, out):
         sb = ctx.enter_context(tc.tile_pool(name="sb", bufs=1))
         on_bias_pool = ctx.enter_context(tc.tile_pool(name="on_bias_pool", bufs=1))
         on_bias_row = ctx.enter_context(tc.tile_pool(name="on_bias_row", bufs=1))
-        on_first_q = ctx.enter_context(tc.tile_pool(name="on_first_q", bufs=1))
         on_scale_pool = ctx.enter_context(tc.tile_pool(name="on_scale_pool", bufs=1))
+        on_first_q = ctx.enter_context(tc.tile_pool(name="on_first_q", bufs=1))
         on_second_q = ctx.enter_context(tc.tile_pool(name="on_second_q", bufs=1))
-        on_third_q = ctx.enter_context(tc.tile_pool(name="on_third_q", bufs=1))
         ps = ctx.enter_context(tc.psum_pool(name="ps", bufs=1))
 
         ident = sb.tile([P, P], F32, name="ident")
@@ -50,17 +50,13 @@ def tile_attend_splade_topk_kernel(tc, qT, k_words, k_scales, kb, offs, out):
         offsets = sb.tile([P, N // 16], U16, name="offsets")
         nc.sync.dma_start(offsets[:], offs)
 
-        scale_pool = on_scale_pool.tile([P, T], U8, name="scale_pool", align_bytes=64, offset=0)
-        nc.sync.dma_start(
-            out=scale_pool[96:P, :].bitcast(I32),
-            in_=k_scales.bitcast(I32).rearrange("o f t -> f o t"),
-        )
-        nc.vector.memset(scale_pool[0:96, :].bitcast(I32), 0)
-
         bias_pool = on_bias_pool.tile([P, T], F32, name="bias_pool", align_bytes=64, offset=0)
         nc.sync.dma_start(out=bias_pool[P - 1 : P, :], in_=kb[0:1, :])
-        nc.vector.memset(bias_pool[0 : P - 1, 0:1280].bitcast(I32), 0)
-        nc.gpsimd.memset(bias_pool[0 : P - 1, 1280:T].bitcast(I32), 0)
+        scale_pool = on_scale_pool.tile([P, T], U8, name="scale_pool", align_bytes=64, offset=T - 64)
+        nc.sync.dma_start(out=scale_pool[96:P, :].bitcast(I32), in_=k_scales.bitcast(I32).rearrange("o f t -> f o t"))
+        for first, last in ((0, 479), (479, 960), (960, T)):
+            nc.vector.memset(bias_pool[0 : P - 1, first:last].bitcast(I32), 0)
+        nc.vector.memset(scale_pool[0:96, :].bitcast(I32), 0)
 
         word_pool = sb.tile([P, T], U32, name="word_pool")
         nc.sync.dma_start(out=word_pool[:].bitcast(I32), in_=k_words[0].rearrange("p t b -> p (t b)").bitcast(I32))
@@ -68,154 +64,139 @@ def tile_attend_splade_topk_kernel(tc, qT, k_words, k_scales, kb, offs, out):
         q_raw = {
             (0, 0): on_first_q.tile([P, PACK, P], F32, name="q_raw00", align_bytes=64, offset=0),
             (0, 1): on_second_q.tile([P, PACK, P], F32, name="q_raw01", align_bytes=64, offset=0),
-            (1, 0): on_third_q.tile([P, PACK, P], F32, name="q_raw10", align_bytes=64, offset=0),
+            (1, 0): sb.tile([P, PACK, P], F32, name="q_raw10", align_bytes=64),
         }
         for h, o in ((0, 0), (0, 1), (1, 0)):
             nc.sync.dma_start(out=q_raw[h, o][:], in_=q_rows[h, o])
 
-        k_scale = sb.tile([P, PASSES * N], U8, name="k_scale", align_bytes=64)
-        nc.vector.memset(k_scale[:].bitcast(I32), 0)
+        def listed(window, g):
+            return window[:].indirect(offsets[:, g * HALF // 16 : (g + 1) * HALF // 16])
+
+        bias_rows = [on_bias_row.tile([P, HALF], F32, name=f"bias_row{g}", align_bytes=64, offset=4 * HALF * g) for g in range(2)]
+        nc.scalar.activation(bias_rows[1][:], listed(bias_pool, 1), ACT.Copy)
+
         scale_rows = sb.tile([P, N], U8, name="scale_rows", align_bytes=64)
+        nc.vector.tensor_copy(bias_rows[0][:], listed(bias_pool, 0))
         nc.vector.tensor_copy(scale_rows[:], scale_pool[:].indirect(offsets[:]))
+        k_scale = on_scale_pool.tile([P, PASSES * N], U8, name="k_scale", align_bytes=64, offset=T)
         for quad in range(4):
-            (nc.sync, nc.scalar)[quad % 2].dma_start(
+            nc.sync.dma_start(
                 out=k_scale[32 * quad : 32 * quad + 4, :].bitcast(I32),
                 in_=scale_rows[96 + 8 * quad : 96 + 8 * quad + 8, :].bitcast(I32),
             )
         q_raw[1, 1] = on_scale_pool.tile([P, PACK, P], F32, name="q_raw11", align_bytes=64, offset=0)
         nc.sync.dma_start(out=q_raw[1, 1][:], in_=q_rows[1, 1])
 
-        def gather_half(dest, window, g):
-            columns = slice(g * HALF // 16, (g + 1) * HALF // 16)
-            nc.vector.tensor_copy(dest[:, g * HALF : (g + 1) * HALF], window[:].indirect(offsets[:, columns]))
-
-        bias_row = on_bias_row.tile([P, N], F32, name="bias_row", align_bytes=64, offset=0)
-        bias_ps = ps.tile([P, 4, P], F32, name="bias_ps", tag="bank7")
+        columns = []
         for g in range(2):
-            gather_half(bias_row, bias_pool, g)
-        for s in range(4):
-            nc.tensor.transpose(bias_ps[:, s, :], bias_row[:, s * P : (s + 1) * P], ident[:])
-
-        pairs = on_bias_pool.tile([P, N], U32, name="pairs", align_bytes=64, offset=8 * N)
+            turned = ps.tile([P, 2, P], F32, name=f"turned{g}", tag=f"bank{6 + g}")
+            for s in range(2):
+                nc.tensor.transpose(turned[:, s, :], bias_rows[g][:, s * P : (s + 1) * P], ident[:])
+            columns.append(on_bias_row.tile([P, 2], F32, name=f"columns{g}", align_bytes=64, offset=8 * HALF + 64 * g))
+            nc.scalar.copy(out=columns[g][:], in_=turned[:, :, P - 1])
+        padded = on_scale_pool.tile([P, RUNS, 12], F32, name="padded", align_bytes=64, offset=T + PASSES * N)
+        nc.vector.memset(padded[:, :, SEG : SEG + 1], 0.0)
+        spread_ps = [ps.tile([P, HALF], F32, name=f"spread_ps{g}", tag=f"bank{1 + g}") for g in range(2)]
         for g in range(2):
-            gather_half(pairs, word_pool, g)
+            for s in range(2):
+                nc.tensor.transpose(spread_ps[g][:, s * P : (s + 1) * P], columns[g][:, s : s + 1].to_broadcast([P, P]), ident[:])
+        spread = [sb.tile([P, HALF], F32, name="spread0")]
+        nc.scalar.copy(out=spread[0][:], in_=spread_ps[0][:])
+
+        pairs = on_bias_pool.tile([P, N], U32, name="pairs", align_bytes=64, offset=0)
+        for g in range(2):
+            nc.vector.tensor_copy(pairs[:, g * HALF : (g + 1) * HALF], listed(word_pool, g))
         halves = pairs[:].bitcast(U16).rearrange("p (n o) -> p o n", o=PASSES)
 
         k_codes = {
-            (0, 0): on_first_q.tile([P, N], U8, name="k_codes00", align_bytes=64, offset=0),
-            (0, 1): on_first_q.tile([P, N], U8, name="k_codes01", align_bytes=64, offset=N),
-            (1, 0): on_first_q.tile([P, N], U8, name="k_codes10", align_bytes=64, offset=2 * N),
+            (0, 0): sb.tile([P, N], U8, name="k_codes00", align_bytes=64),
+            (0, 1): on_first_q.tile([P, N], U8, name="k_codes01", align_bytes=64, offset=0),
+            (1, 0): on_first_q.tile([P, N], U8, name="k_codes10", align_bytes=64, offset=N),
             (1, 1): on_second_q.tile([P, N], U8, name="k_codes11", align_bytes=64, offset=0),
         }
-        q_bf = {
-            (0, 0): on_bias_pool.tile([P, P, PACK], BF16, name="q_bf00", align_bytes=64, offset=0),
-            (0, 1): on_bias_row.tile([P, P, PACK], BF16, name="q_bf01", align_bytes=64, offset=0),
-            (1, 0): on_bias_row.tile([P, P, PACK], BF16, name="q_bf10", align_bytes=64, offset=2 * N),
-            (1, 1): sb.tile([P, P, PACK], BF16, name="q_bf11", align_bytes=64),
-        }
+        q_cast = on_bias_row.tile([P, 2 * PASSES * P * PACK], BF16, name="q_cast", align_bytes=64, offset=0)
         q_mx = {}
 
         def part_words(o, g):
             nc.vector.tensor_copy(out=k_codes[o, g][:].bitcast(U16), in_=halves[:, o, g * HALF : (g + 1) * HALF])
 
-        def cast(h, o, copy):
-            copy(
-                out=q_bf[h, o][:].rearrange("p (c i) t -> p c t i", i=4),
+        def cast_and_quantise(h, o):
+            first = (PASSES * h + o) * P * PACK
+            q_bf = q_cast[:, first : first + P * PACK]
+            nc.scalar.copy(
+                out=q_bf.rearrange("p (c i t) -> p c t i", i=4, t=PACK),
                 in_=q_raw[h, o][:].rearrange("p t (c i) -> p c t i", i=4),
             )
-
-        def quantise(h, o):
             codes = sb.tile([P, P], U32, name=f"q_codes{h}{o}", align_bytes=64)
             plane = sb.tile([P, P], U8, name=f"q_scale{h}{o}", align_bytes=64)
-            nc.vector.quantize_mx(out=codes[:].bitcast(FP8X4), scales=plane[:], in_=q_bf[h, o][:].rearrange("p w t -> p (w t)"))
+            nc.vector.quantize_mx(out=codes[:].bitcast(FP8X4), scales=plane[:], in_=q_bf)
             q_mx[h, o] = codes[:].bitcast(FP8X4), plane[:]
 
-        def keys(o, s):
-            return k_codes[o, s // 2][:, 2 * P * (s % 2) : 2 * P * (s % 2 + 1)].bitcast(FP4X4), k_scale[:, o * N + s * P : o * N + (s + 1) * P]
+        scores = {(h, g): ps.tile([P, HALF], F32, name=f"scores{h}{g}", tag=f"bank{(0, 3, 4, 5)[2 * h + g]}") for h in range(2) for g in range(2)}
 
-        def product(bank, stationary, moving, o):
-            nc.tensor.matmul_mx(
-                out=bank[:],
-                lhsT=stationary[0],
-                lhsT_scale=stationary[1],
-                rhs=moving[0],
-                rhs_scale=moving[1],
-                start=(o == 0),
-                stop=(o == 1),
+        def products(h, o):
+            for g in range(2):
+                nc.tensor.matmul_mx(
+                    out=scores[h, g][:],
+                    lhsT=q_mx[h, o][0],
+                    lhsT_scale=q_mx[h, o][1],
+                    rhs=k_codes[o, g][:].bitcast(FP4X4),
+                    rhs_scale=k_scale[:, o * N + g * HALF : o * N + (g + 1) * HALF],
+                    start=(o == 0),
+                    stop=(o == 1),
+                )
+
+        def add_bias(h, g, biased):
+            runs = [tile[:].rearrange("p (j e) -> p j e", e=SEG) for tile in (scores[h, g], spread[g])]
+            nc.vector.tensor_tensor(biased[:, :, 0:SEG], runs[0], runs[1], ALU.add)
+
+        def largest(best, g, biased):
+            nc.vector.tensor_reduce(
+                out=best[:, g * HALF // SEG : (g + 1) * HALF // SEG],
+                in_=biased,
+                axis=mybir.AxisListType.X,
+                op=ALU.max,
             )
 
-        cast(0, 0, nc.scalar.copy)
-        quantise(0, 0)
-        bias_col = sb.tile([P, 4], F32, name="bias_col", tag="bias_col")
-        nc.scalar.copy(out=bias_col[:], in_=bias_ps[:, :, P - 1])
+        def finish(h, clipped):
+            result = sb.tile([P, RUNS], F32, name=f"result{h}")
+            nc.scalar.activation(result[:], clipped[:], ACT.Ln, bias=1.0)
+            nc.sync.dma_start(out=out[0, h * P : (h + 1) * P, :], in_=result[:])
+
         part_words(0, 0)
+        cast_and_quantise(0, 0)
         part_words(0, 1)
         part_words(1, 0)
-        cast(0, 1, nc.scalar.copy)
-        quantise(0, 1)
+        cast_and_quantise(0, 1)
         part_words(1, 1)
-        cast(1, 0, nc.scalar.copy)
-        quantise(1, 0)
-        cast(1, 1, nc.scalar.copy)
+        spread.append(on_second_q.tile([P, HALF], F32, name="spread1", align_bytes=64, offset=2 * N))
+        nc.vector.tensor_copy(out=spread[1][:], in_=spread_ps[1][:])
+        products(0, 0)
+        products(0, 1)
+        cast_and_quantise(1, 0)
+        products(1, 0)
 
-        spread = [
-            on_third_q.tile([P, HALF], F32, name="spread0", align_bytes=64, offset=0),
-            on_scale_pool.tile([P, HALF], F32, name="spread1", align_bytes=64, offset=0),
+        biased = {
+            (0, 0): sb.tile([P, RUNS // 2, SEG], F32, name="biased00")[:],
+            (0, 1): on_scale_pool.tile([P, RUNS // 2, SEG], F32, name="biased01", align_bytes=64, offset=0)[:],
+            (1, 0): padded[:, 0 : RUNS // 2, 0 : SEG + 1],
+            (1, 1): padded[:, RUNS // 2 : RUNS, 0 : SEG + 1],
+        }
+        best = [
+            on_scale_pool.tile([P, RUNS], F32, name="best0", align_bytes=64, offset=4 * HALF),
+            sb.tile([P, RUNS], F32, name="best1"),
         ]
-        spread_ps = ps.tile([P, N], F32, name="spread_ps", tag="bank5")
-        for s in range(4):
-            nc.tensor.transpose(spread_ps[:, s * P : (s + 1) * P], bias_col[:, s : s + 1].to_broadcast([P, P]), ident[:])
-        for g, copy in enumerate((nc.vector.tensor_copy, nc.scalar.copy)):
-            copy(out=spread[g][:], in_=spread_ps[:, g * HALF : (g + 1) * HALF])
-
-        by_query = [ps.tile([P, P], F32, name=f"by_query{s}", tag=f"bank{(7, 1, 2, 3)[s]}") for s in range(4)]
-        for o in range(PASSES):
-            for s in range(4):
-                product(by_query[s], q_mx[0, o], keys(o, s), o)
-
-        biased = on_scale_pool.tile([P, N], F32, name="biased", align_bytes=64, offset=2 * N)
-
-        def add_bias(s):
-            slots = slice(s * P, (s + 1) * P)
-            nc.vector.tensor_tensor(biased[:, slots], by_query[s][:], spread[s // 2][:, (s % 2) * P : (s % 2 + 1) * P], ALU.add)
-
-        quantise(1, 1)
-        for s in range(4):
-            add_bias(s)
-        best_rows = sb.tile([P, N // SEG], F32, name="best_rows")
+        add_bias(0, 0, biased[0, 0])
+        cast_and_quantise(1, 1)
+        products(1, 1)
+        add_bias(0, 1, biased[0, 1])
         for g in range(2):
-            nc.vector.tensor_reduce(
-                out=best_rows[:, g * HALF // SEG : (g + 1) * HALF // SEG],
-                in_=biased[:, g * HALF : (g + 1) * HALF].rearrange("p (j e) -> p j e", e=SEG),
-                axis=mybir.AxisListType.X,
-                op=ALU.max,
-            )
-
-        by_slot = [ps.tile([P, P], F32, name=f"by_slot{s}", tag=f"bank{(0, 6, 4, 5)[s]}") for s in range(4)]
-        acts = {}
-        for s, o in ((0, 0), (1, 0), (2, 0), (0, 1), (3, 0), (1, 1), (2, 1), (3, 1)):
-            product(by_slot[s], keys(o, s), q_mx[1, o], o)
-            if o == 1:
-                acts[s] = sb.tile([P, P], F32, name=f"act{s}")
-                nc.scalar.activation(acts[s][:], by_slot[s][:], ACT.Relu, bias=bias_col[:, s : s + 1])
-
-        clipped = sb.tile([P, N // SEG], F32, name="clipped", tag="bias_col")
-        nc.scalar.activation(clipped[:], best_rows[:], ACT.Relu)
-        result_rows = sb.tile([P, N // SEG], F32, name="result_rows")
-        nc.scalar.activation(result_rows[:], clipped[:], ACT.Ln, bias=1.0)
-        nc.sync.dma_start(out=out[0, 0:P, :], in_=result_rows[:])
-
-        best = on_scale_pool.tile([P, N // SEG], F32, name="best", align_bytes=64, offset=5 * N)
-        for first, count, bank in ((0, 2, 7), (2, 1, 1), (3, 1, 2)):
-            turned = ps.tile([P, count * P], F32, name=f"turned{first}", tag=f"bank{bank}")
-            for i in range(count):
-                nc.tensor.transpose(turned[:, i * P : (i + 1) * P], acts[first + i][:], ident[:])
-            nc.vector.tensor_reduce(
-                out=best[:, first * P // SEG : (first + count) * P // SEG],
-                in_=turned[:].rearrange("p (j e) -> p j e", e=SEG),
-                axis=mybir.AxisListType.X,
-                op=ALU.max,
-            )
-        result = sb.tile([P, N // SEG], F32, name="result")
-        nc.scalar.activation(result[:], best[:], ACT.Ln, bias=1.0)
-        nc.sync.dma_start(out=out[0, P : 2 * P, :], in_=result[:])
+            largest(best[0], g, biased[0, g])
+        for g in range(2):
+            add_bias(1, g, biased[1, g])
+        clipped = sb.tile([P, RUNS], F32, name="clipped")
+        nc.scalar.activation(clipped[:], best[0][:], ACT.Relu)
+        finish(0, clipped)
+        for g in range(2):
+            largest(best[1], g, biased[1, g])
+        finish(1, best[1])

@@ -87,21 +87,24 @@ def tile_attend_splade_topk_kernel(tc, qT, k_words, k_scales, kb, offs, out):
         q_raw[1, 1] = on_scale_pool.tile([P, PACK, P], F32, name="q_raw11", align_bytes=64, offset=0)
         nc.sync.dma_start(out=q_raw[1, 1][:], in_=q_rows[1, 1])
 
+        pieces = ((0, 1), (1, 1), (2, 2))
         columns = []
-        for g in range(2):
-            turned = ps.tile([P, 2, P], F32, name=f"turned{g}", tag=f"bank{6 + g}")
-            for s in range(2):
-                nc.tensor.transpose(turned[:, s, :], bias_rows[g][:, s * P : (s + 1) * P], ident[:])
-            columns.append(on_bias_row.tile([P, 2], F32, name=f"columns{g}", align_bytes=64, offset=8 * HALF + 64 * g))
-            nc.scalar.copy(out=columns[g][:], in_=turned[:, :, P - 1])
+        for i, (first, count) in enumerate(pieces):
+            turned = ps.tile([P, count, P], F32, name=f"turned{i}", tag=f"bank{(0, 4, 6)[i]}")
+            for s in range(first, first + count):
+                nc.tensor.transpose(turned[:, s - first, :], bias_rows[s // 2][:, (s % 2) * P : (s % 2 + 1) * P], ident[:])
+            columns.append(on_bias_row.tile([P, count], F32, name=f"columns{i}", align_bytes=64, offset=(8 * HALF, 8 * HALF + 64, 16 * HALF)[i]))
+            nc.scalar.copy(out=columns[i][:], in_=turned[:, :, P - 1])
         padded = on_scale_pool.tile([P, RUNS, 12], F32, name="padded", align_bytes=64, offset=T + PASSES * N)
-        nc.vector.memset(padded[:, :, SEG : SEG + 1], 0.0)
-        spread_ps = [ps.tile([P, HALF], F32, name=f"spread_ps{g}", tag=f"bank{1 + g}") for g in range(2)]
-        for g in range(2):
-            for s in range(2):
-                nc.tensor.transpose(spread_ps[g][:, s * P : (s + 1) * P], columns[g][:, s : s + 1].to_broadcast([P, P]), ident[:])
+        nc.vector.memset(padded[:, :, SEG:12], 0.0)
         spread = [sb.tile([P, HALF], F32, name="spread0")]
-        nc.scalar.copy(out=spread[0][:], in_=spread_ps[0][:])
+        spread_ps = []
+        for i, (first, count) in enumerate(pieces):
+            spread_ps.append(ps.tile([P, count * P], F32, name=f"spread_ps{i}", tag=f"bank{(1, 5, 2)[i]}"))
+            for s in range(count):
+                nc.tensor.transpose(spread_ps[i][:, s * P : (s + 1) * P], columns[i][:, s : s + 1].to_broadcast([P, P]), ident[:])
+            if count == 1:
+                nc.scalar.copy(out=spread[0][:, first * P : (first + 1) * P], in_=spread_ps[i][:])
 
         pairs = on_bias_pool.tile([P, N], U32, name="pairs", align_bytes=64, offset=0)
         for g in range(2):
@@ -170,7 +173,7 @@ def tile_attend_splade_topk_kernel(tc, qT, k_words, k_scales, kb, offs, out):
         cast_and_quantise(0, 1)
         part_words(1, 1)
         spread.append(on_second_q.tile([P, HALF], F32, name="spread1", align_bytes=64, offset=2 * N))
-        nc.vector.tensor_copy(out=spread[1][:], in_=spread_ps[1][:])
+        nc.vector.tensor_copy(out=spread[1][:], in_=spread_ps[2][:])
         products(0, 0)
         products(0, 1)
         cast_and_quantise(1, 0)

@@ -113,7 +113,7 @@ def tile_attend_splade_topk_kernel(tc, qT, k_words, k_scales, kb, offs, out):
 
         k_codes = {
             (0, 0): sb.tile([P, N], U8, name="k_codes00", align_bytes=64),
-            (0, 1): on_first_q.tile([P, N], U8, name="k_codes01", align_bytes=64, offset=0),
+            (0, 1): on_second_q.tile([P, N], U8, name="k_codes01", align_bytes=64, offset=N),
             (1, 0): on_first_q.tile([P, N], U8, name="k_codes10", align_bytes=64, offset=N),
             (1, 1): on_second_q.tile([P, N], U8, name="k_codes11", align_bytes=64, offset=0),
         }
@@ -137,17 +137,16 @@ def tile_attend_splade_topk_kernel(tc, qT, k_words, k_scales, kb, offs, out):
 
         scores = {(h, g): ps.tile([P, HALF], F32, name=f"scores{h}{g}", tag=f"bank{(0, 3, 4, 5)[2 * h + g]}") for h in range(2) for g in range(2)}
 
-        def products(h, o):
-            for g in range(2):
-                nc.tensor.matmul_mx(
-                    out=scores[h, g][:],
-                    lhsT=q_mx[h, o][0],
-                    lhsT_scale=q_mx[h, o][1],
-                    rhs=k_codes[o, g][:].bitcast(FP4X4),
-                    rhs_scale=k_scale[:, o * N + g * HALF : o * N + (g + 1) * HALF],
-                    start=(o == 0),
-                    stop=(o == 1),
-                )
+        def product(h, o, g):
+            nc.tensor.matmul_mx(
+                out=scores[h, g][:],
+                lhsT=q_mx[h, o][0],
+                lhsT_scale=q_mx[h, o][1],
+                rhs=k_codes[o, g][:].bitcast(FP4X4),
+                rhs_scale=k_scale[:, o * N + g * HALF : o * N + (g + 1) * HALF],
+                start=(o == 0),
+                stop=(o == 1),
+            )
 
         def add_bias(h, g, biased):
             runs = [tile[:].rearrange("p (j e) -> p j e", e=SEG) for tile in (scores[h, g], spread[g])]
@@ -168,16 +167,18 @@ def tile_attend_splade_topk_kernel(tc, qT, k_words, k_scales, kb, offs, out):
 
         part_words(0, 0)
         cast_and_quantise(0, 0)
-        part_words(0, 1)
         part_words(1, 0)
         cast_and_quantise(0, 1)
+        part_words(0, 1)
         part_words(1, 1)
         spread.append(on_second_q.tile([P, HALF], F32, name="spread1", align_bytes=64, offset=2 * N))
         nc.vector.tensor_copy(out=spread[1][:], in_=spread_ps[2][:])
-        products(0, 0)
-        products(0, 1)
+        for g in range(2):
+            for o in range(PASSES):
+                product(0, o, g)
         cast_and_quantise(1, 0)
-        products(1, 0)
+        for g in range(2):
+            product(1, 0, g)
 
         biased = {
             (0, 0): sb.tile([P, RUNS // 2, SEG], F32, name="biased00")[:],
@@ -191,7 +192,8 @@ def tile_attend_splade_topk_kernel(tc, qT, k_words, k_scales, kb, offs, out):
         ]
         add_bias(0, 0, biased[0, 0])
         cast_and_quantise(1, 1)
-        products(1, 1)
+        for g in range(2):
+            product(1, 1, g)
         add_bias(0, 1, biased[0, 1])
         for g in range(2):
             largest(best[0], g, biased[0, g])

@@ -1,7 +1,6 @@
 from contextlib import ExitStack
 
 import concourse.mybir as mybir
-from concourse.masks import make_identity
 
 F32 = mybir.dt.float32
 BF16 = mybir.dt.bfloat16
@@ -40,8 +39,8 @@ def tile_attend_splade_topk_kernel(tc, qT, k_words, k_scales, kb, offs, out):
         on_second_q = ctx.enter_context(tc.tile_pool(name="on_second_q", bufs=1))
         ps = ctx.enter_context(tc.psum_pool(name="ps", bufs=1))
 
-        ident = sb.tile([P, P], F32, name="ident")
-        make_identity(nc, ident[:])
+        distance = sb.tile([P, P], I32, name="distance")
+        nc.gpsimd.iota(distance[:], [[1, P]], base=0, channel_multiplier=-1)
         zero = sb.tile([P, 1], F32, name="zero")
         nc.vector.memset(zero[:], 0.0)
         warm = sb.tile([P, 1], F32, name="warm")
@@ -54,9 +53,8 @@ def tile_attend_splade_topk_kernel(tc, qT, k_words, k_scales, kb, offs, out):
         nc.sync.dma_start(out=bias_pool[P - 1 : P, :], in_=kb[0:1, :])
         scale_pool = on_scale_pool.tile([P, T], U8, name="scale_pool", align_bytes=64, offset=T - 64)
         nc.sync.dma_start(out=scale_pool[96:P, :].bitcast(I32), in_=k_scales.bitcast(I32).rearrange("o f t -> f o t"))
-        for first, last in ((0, 479), (479, 960), (960, T)):
-            nc.vector.memset(bias_pool[0 : P - 1, first:last].bitcast(I32), 0)
         nc.vector.memset(scale_pool[0:96, :].bitcast(I32), 0)
+        nc.vector.memset(bias_pool[0 : P - 1, :].bitcast(I32), 0)
 
         word_pool = sb.tile([P, T], U32, name="word_pool")
         nc.sync.dma_start(out=word_pool[:].bitcast(I32), in_=k_words[0].rearrange("p t b -> p (t b)").bitcast(I32))
@@ -69,14 +67,17 @@ def tile_attend_splade_topk_kernel(tc, qT, k_words, k_scales, kb, offs, out):
         for h, o in ((0, 0), (0, 1), (1, 0)):
             nc.sync.dma_start(out=q_raw[h, o][:], in_=q_rows[h, o])
 
-        def listed(window, g):
-            return window[:].indirect(offsets[:, g * HALF // 16 : (g + 1) * HALF // 16])
+        def listed(window, first, count):
+            return window[:].indirect(offsets[:, first // 16 : (first + count) // 16])
 
         bias_rows = [on_bias_row.tile([P, HALF], F32, name=f"bias_row{g}", align_bytes=64, offset=4 * HALF * g) for g in range(2)]
-        nc.scalar.activation(bias_rows[1][:], listed(bias_pool, 1), ACT.Copy)
+        nc.scalar.activation(bias_rows[1][:, 0:P], listed(bias_pool, HALF, P), ACT.Copy)
+        ident = sb.tile([P, P], F32, name="ident")
+        nc.scalar.activation(ident[:], distance[:].bitcast(U32), ACT.Relu, scale=-1.0, bias=1.0)
 
         scale_rows = sb.tile([P, N], U8, name="scale_rows", align_bytes=64)
-        nc.vector.tensor_copy(bias_rows[0][:], listed(bias_pool, 0))
+        nc.vector.tensor_copy(bias_rows[0][:], listed(bias_pool, 0, HALF))
+        nc.vector.tensor_copy(bias_rows[1][:, P:HALF], listed(bias_pool, HALF + P, P))
         nc.vector.tensor_copy(scale_rows[:], scale_pool[:].indirect(offsets[:]))
         k_scale = on_scale_pool.tile([P, PASSES * N], U8, name="k_scale", align_bytes=64, offset=T)
         for quad in range(4):
@@ -108,7 +109,7 @@ def tile_attend_splade_topk_kernel(tc, qT, k_words, k_scales, kb, offs, out):
 
         pairs = on_bias_pool.tile([P, N], U32, name="pairs", align_bytes=64, offset=0)
         for g in range(2):
-            nc.vector.tensor_copy(pairs[:, g * HALF : (g + 1) * HALF], listed(word_pool, g))
+            nc.vector.tensor_copy(pairs[:, g * HALF : (g + 1) * HALF], listed(word_pool, g * HALF, HALF))
         halves = pairs[:].bitcast(U16).rearrange("p (n o) -> p o n", o=PASSES)
 
         k_codes = {
@@ -123,13 +124,15 @@ def tile_attend_splade_topk_kernel(tc, qT, k_words, k_scales, kb, offs, out):
         def part_words(o, g):
             nc.vector.tensor_copy(out=k_codes[o, g][:].bitcast(U16), in_=halves[:, o, g * HALF : (g + 1) * HALF])
 
-        def cast_and_quantise(h, o):
-            first = (PASSES * h + o) * P * PACK
-            q_bf = q_cast[:, first : first + P * PACK]
-            nc.scalar.copy(
-                out=q_bf.rearrange("p (c i t) -> p c t i", i=4, t=PACK),
-                in_=q_raw[h, o][:].rearrange("p t (c i) -> p c t i", i=4),
+        def cast(copy, h, o, first, last):
+            q_bf = q_cast[:, (PASSES * h + o) * P * PACK : (PASSES * h + o + 1) * P * PACK]
+            copy(
+                out=q_bf.rearrange("p (c i t) -> p c t i", i=4, t=PACK)[:, first // 4 : last // 4],
+                in_=q_raw[h, o][:].rearrange("p t (c i) -> p c t i", i=4)[:, first // 4 : last // 4],
             )
+
+        def quantise(h, o):
+            q_bf = q_cast[:, (PASSES * h + o) * P * PACK : (PASSES * h + o + 1) * P * PACK]
             codes = sb.tile([P, P], U32, name=f"q_codes{h}{o}", align_bytes=64)
             plane = sb.tile([P, P], U8, name=f"q_scale{h}{o}", align_bytes=64)
             nc.vector.quantize_mx(out=codes[:].bitcast(FP8X4), scales=plane[:], in_=q_bf)
@@ -166,9 +169,12 @@ def tile_attend_splade_topk_kernel(tc, qT, k_words, k_scales, kb, offs, out):
             nc.sync.dma_start(out=out[0, h * P : (h + 1) * P, :], in_=result[:])
 
         part_words(0, 0)
-        cast_and_quantise(0, 0)
+        cast(nc.scalar.copy, 0, 0, 0, P)
+        quantise(0, 0)
+        cast(nc.scalar.copy, 0, 1, 0, P // 2)
+        cast(nc.vector.tensor_copy, 0, 1, P // 2, P)
         part_words(1, 0)
-        cast_and_quantise(0, 1)
+        quantise(0, 1)
         part_words(0, 1)
         part_words(1, 1)
         spread.append(on_second_q.tile([P, HALF], F32, name="spread1", align_bytes=64, offset=2 * N))
@@ -176,7 +182,8 @@ def tile_attend_splade_topk_kernel(tc, qT, k_words, k_scales, kb, offs, out):
         for g in range(2):
             for o in range(PASSES):
                 product(0, o, g)
-        cast_and_quantise(1, 0)
+        cast(nc.scalar.copy, 1, 0, 0, P)
+        quantise(1, 0)
         for g in range(2):
             product(1, 0, g)
 
@@ -191,7 +198,8 @@ def tile_attend_splade_topk_kernel(tc, qT, k_words, k_scales, kb, offs, out):
             sb.tile([P, RUNS], F32, name="best1"),
         ]
         add_bias(0, 0, biased[0, 0])
-        cast_and_quantise(1, 1)
+        cast(nc.scalar.copy, 1, 1, 0, P)
+        quantise(1, 1)
         for g in range(2):
             product(1, 1, g)
         add_bias(0, 1, biased[0, 1])

from contextlib import ExitStack

import concourse.mybir as mybir

F32 = mybir.dt.float32
BF16 = mybir.dt.bfloat16
I32 = mybir.dt.int32
U32 = mybir.dt.uint32
U16 = mybir.dt.uint16
U8 = mybir.dt.uint8
FP8X4 = mybir.dt.float8_e4m3fn_x4
FP4X4 = mybir.dt.float4_e2m1fn_x4
ACT = mybir.ActivationFunctionType
ALU = mybir.AluOpType

P = 128
PACK = 4
PASSES = 2
D = 1024
NQ = 256
N = 512
T = 2048
SEG = 8
HALF = N // 2
RUNS = N // SEG

FLOPS = 2 * NQ * N * D
BYTES = D * NQ * 4 + P * T * 4 + PASSES * 16 * T + T * 4 + P * (N // 16) * 2 + NQ * (N // SEG) * 4


def tile_attend_splade_topk_kernel(tc, qT, k_words, k_scales, kb, offs, out):
    nc = tc.nc
    with ExitStack() as ctx:
        sb = ctx.enter_context(tc.tile_pool(name="sb", bufs=1))
        on_bias_pool = ctx.enter_context(tc.tile_pool(name="on_bias_pool", bufs=1))
        on_bias_row = ctx.enter_context(tc.tile_pool(name="on_bias_row", bufs=1))
        on_scale_pool = ctx.enter_context(tc.tile_pool(name="on_scale_pool", bufs=1))
        on_first_q = ctx.enter_context(tc.tile_pool(name="on_first_q", bufs=1))
        on_second_q = ctx.enter_context(tc.tile_pool(name="on_second_q", bufs=1))
        ps = ctx.enter_context(tc.psum_pool(name="ps", bufs=1))

        distance = sb.tile([P, P], I32, name="distance")
        nc.gpsimd.iota(distance[:], [[1, P]], base=0, channel_multiplier=-1)
        zero = sb.tile([P, 1], F32, name="zero")
        nc.vector.memset(zero[:], 0.0)
        warm = sb.tile([P, 1], F32, name="warm")
        nc.scalar.activation(warm[:], zero[:], ACT.Ln, bias=1.0)

        offsets = sb.tile([P, N // 16], U16, name="offsets")
        nc.sync.dma_start(offsets[:], offs)

        bias_pool = on_bias_pool.tile([P, T], F32, name="bias_pool", align_bytes=64, offset=0)
        nc.sync.dma_start(out=bias_pool[P - 1 : P, :], in_=kb[0:1, :])
        scale_pool = on_scale_pool.tile([P, T], U8, name="scale_pool", align_bytes=64, offset=T - 64)
        nc.sync.dma_start(out=scale_pool[96:P, :].bitcast(I32), in_=k_scales.bitcast(I32).rearrange("o f t -> f o t"))
        nc.vector.memset(scale_pool[0:96, :].bitcast(I32), 0)
        nc.vector.memset(bias_pool[0 : P - 1, :].bitcast(I32), 0)

        word_pool = sb.tile([P, T], U32, name="word_pool")
        nc.sync.dma_start(out=word_pool[:].bitcast(I32), in_=k_words[0].rearrange("p t b -> p (t b)").bitcast(I32))
        q_rows = qT[0].rearrange("(o p j) (h w) -> h o p j w", o=PASSES, j=PACK, h=2)
        q_raw = {
            (0, 0): on_first_q.tile([P, PACK, P], F32, name="q_raw00", align_bytes=64, offset=0),
            (0, 1): on_second_q.tile([P, PACK, P], F32, name="q_raw01", align_bytes=64, offset=0),
            (1, 0): sb.tile([P, PACK, P], F32, name="q_raw10", align_bytes=64),
        }
        for h, o in ((0, 0), (0, 1), (1, 0)):
            nc.sync.dma_start(out=q_raw[h, o][:], in_=q_rows[h, o])

        def listed(window, first, count):
            return window[:].indirect(offsets[:, first // 16 : (first + count) // 16])

        bias_rows = [on_bias_row.tile([P, HALF], F32, name=f"bias_row{g}", align_bytes=64, offset=4 * HALF * g) for g in range(2)]
        nc.scalar.activation(bias_rows[1][:, 0:P], listed(bias_pool, HALF, P), ACT.Copy)
        ident = sb.tile([P, P], F32, name="ident")
        nc.scalar.activation(ident[:], distance[:].bitcast(U32), ACT.Relu, scale=-1.0, bias=1.0)

        scale_rows = sb.tile([P, N], U8, name="scale_rows", align_bytes=64)
        nc.vector.tensor_copy(bias_rows[0][:], listed(bias_pool, 0, HALF))
        nc.vector.tensor_copy(bias_rows[1][:, P:HALF], listed(bias_pool, HALF + P, P))
        nc.vector.tensor_copy(scale_rows[:], scale_pool[:].indirect(offsets[:]))
        k_scale = on_scale_pool.tile([P, PASSES * N], U8, name="k_scale", align_bytes=64, offset=T)
        for quad in range(4):
            nc.sync.dma_start(
                out=k_scale[32 * quad : 32 * quad + 4, :].bitcast(I32),
                in_=scale_rows[96 + 8 * quad : 96 + 8 * quad + 8, :].bitcast(I32),
            )
        q_raw[1, 1] = on_scale_pool.tile([P, PACK, P], F32, name="q_raw11", align_bytes=64, offset=0)
        nc.sync.dma_start(out=q_raw[1, 1][:], in_=q_rows[1, 1])

        pieces = ((0, 1), (1, 1), (2, 2))
        columns = []
        for i, (first, count) in enumerate(pieces):
            turned = ps.tile([P, count, P], F32, name=f"turned{i}", tag=f"bank{(0, 4, 6)[i]}")
            for s in range(first, first + count):
                nc.tensor.transpose(turned[:, s - first, :], bias_rows[s // 2][:, (s % 2) * P : (s % 2 + 1) * P], ident[:])
            columns.append(on_bias_row.tile([P, count], F32, name=f"columns{i}", align_bytes=64, offset=(8 * HALF, 8 * HALF + 64, 16 * HALF)[i]))
            nc.scalar.copy(out=columns[i][:], in_=turned[:, :, P - 1])
        padded = on_scale_pool.tile([P, RUNS, 12], F32, name="padded", align_bytes=64, offset=T + PASSES * N)
        nc.vector.memset(padded[:, :, SEG:12], 0.0)
        spread = [sb.tile([P, HALF], F32, name="spread0")]
        spread_ps = []
        for i, (first, count) in enumerate(pieces):
            spread_ps.append(ps.tile([P, count * P], F32, name=f"spread_ps{i}", tag=f"bank{(1, 5, 2)[i]}"))
            for s in range(count):
                nc.tensor.transpose(spread_ps[i][:, s * P : (s + 1) * P], columns[i][:, s : s + 1].to_broadcast([P, P]), ident[:])
            if count == 1:
                nc.scalar.copy(out=spread[0][:, first * P : (first + 1) * P], in_=spread_ps[i][:])

        pairs = on_bias_pool.tile([P, N], U32, name="pairs", align_bytes=64, offset=0)
        for g in range(2):
            nc.vector.tensor_copy(pairs[:, g * HALF : (g + 1) * HALF], listed(word_pool, g * HALF, HALF))
        halves = pairs[:].bitcast(U16).rearrange("p (n o) -> p o n", o=PASSES)

        k_codes = {
            (0, 0): sb.tile([P, N], U8, name="k_codes00", align_bytes=64),
            (0, 1): on_second_q.tile([P, N], U8, name="k_codes01", align_bytes=64, offset=N),
            (1, 0): on_first_q.tile([P, N], U8, name="k_codes10", align_bytes=64, offset=N),
            (1, 1): on_second_q.tile([P, N], U8, name="k_codes11", align_bytes=64, offset=0),
        }
        q_cast = on_bias_row.tile([P, 2 * PASSES * P * PACK], BF16, name="q_cast", align_bytes=64, offset=0)
        q_mx = {}

        def part_words(o, g):
            nc.vector.tensor_copy(out=k_codes[o, g][:].bitcast(U16), in_=halves[:, o, g * HALF : (g + 1) * HALF])

        def cast(copy, h, o, first, last):
            q_bf = q_cast[:, (PASSES * h + o) * P * PACK : (PASSES * h + o + 1) * P * PACK]
            copy(
                out=q_bf.rearrange("p (c i t) -> p c t i", i=4, t=PACK)[:, first // 4 : last // 4],
                in_=q_raw[h, o][:].rearrange("p t (c i) -> p c t i", i=4)[:, first // 4 : last // 4],
            )

        def quantise(h, o):
            q_bf = q_cast[:, (PASSES * h + o) * P * PACK : (PASSES * h + o + 1) * P * PACK]
            codes = sb.tile([P, P], U32, name=f"q_codes{h}{o}", align_bytes=64)
            plane = sb.tile([P, P], U8, name=f"q_scale{h}{o}", align_bytes=64)
            nc.vector.quantize_mx(out=codes[:].bitcast(FP8X4), scales=plane[:], in_=q_bf)
            q_mx[h, o] = codes[:].bitcast(FP8X4), plane[:]

        scores = {(h, g): ps.tile([P, HALF], F32, name=f"scores{h}{g}", tag=f"bank{(0, 3, 4, 5)[2 * h + g]}") for h in range(2) for g in range(2)}

        def product(h, o, g):
            nc.tensor.matmul_mx(
                out=scores[h, g][:],
                lhsT=q_mx[h, o][0],
                lhsT_scale=q_mx[h, o][1],
                rhs=k_codes[o, g][:].bitcast(FP4X4),
                rhs_scale=k_scale[:, o * N + g * HALF : o * N + (g + 1) * HALF],
                start=(o == 0),
                stop=(o == 1),
            )

        def add_bias(h, g, biased):
            runs = [tile[:].rearrange("p (j e) -> p j e", e=SEG) for tile in (scores[h, g], spread[g])]
            nc.vector.tensor_tensor(biased[:, :, 0:SEG], runs[0], runs[1], ALU.add)

        def largest(best, g, biased):
            nc.vector.tensor_reduce(
                out=best[:, g * HALF // SEG : (g + 1) * HALF // SEG],
                in_=biased,
                axis=mybir.AxisListType.X,
                op=ALU.max,
            )

        def finish(h, clipped):
            result = sb.tile([P, RUNS], F32, name=f"result{h}")
            nc.scalar.activation(result[:], clipped[:], ACT.Ln, bias=1.0)
            nc.sync.dma_start(out=out[0, h * P : (h + 1) * P, :], in_=result[:])

        part_words(0, 0)
        cast(nc.scalar.copy, 0, 0, 0, P)
        quantise(0, 0)
        cast(nc.scalar.copy, 0, 1, 0, P // 2)
        cast(nc.vector.tensor_copy, 0, 1, P // 2, P)
        part_words(1, 0)
        quantise(0, 1)
        part_words(0, 1)
        part_words(1, 1)
        spread.append(on_second_q.tile([P, HALF], F32, name="spread1", align_bytes=64, offset=2 * N))
        nc.vector.tensor_copy(out=spread[1][:], in_=spread_ps[2][:])
        for g in range(2):
            for o in range(PASSES):
                product(0, o, g)
        cast(nc.scalar.copy, 1, 0, 0, P)
        quantise(1, 0)
        for g in range(2):
            product(1, 0, g)

        biased = {
            (0, 0): sb.tile([P, RUNS // 2, SEG], F32, name="biased00")[:],
            (0, 1): on_scale_pool.tile([P, RUNS // 2, SEG], F32, name="biased01", align_bytes=64, offset=0)[:],
            (1, 0): padded[:, 0 : RUNS // 2, 0 : SEG + 1],
            (1, 1): padded[:, RUNS // 2 : RUNS, 0 : SEG + 1],
        }
        best = [
            on_scale_pool.tile([P, RUNS], F32, name="best0", align_bytes=64, offset=4 * HALF),
            sb.tile([P, RUNS], F32, name="best1"),
        ]
        add_bias(0, 0, biased[0, 0])
        cast(nc.scalar.copy, 1, 1, 0, P)
        quantise(1, 1)
        for g in range(2):
            product(1, 1, g)
        add_bias(0, 1, biased[0, 1])
        for g in range(2):
            largest(best[0], g, biased[0, g])
        for g in range(2):
            add_bias(1, g, biased[1, g])
        clipped = sb.tile([P, RUNS], F32, name="clipped")
        nc.scalar.activation(clipped[:], best[0][:], ACT.Relu)
        finish(0, clipped)
        for g in range(2):
            largest(best[1], g, biased[1, g])
        finish(1, best[1])
